import numpy as np
import ml_dtypes


def mxq(x, axis, fmt="e4m3"):
    dtype, down = {"e4m3": (ml_dtypes.float8_e4m3fn, 7), "e5m2": (ml_dtypes.float8_e5m2, 14)}[fmt]
    v = np.moveaxis(np.asarray(x, np.float32).astype(ml_dtypes.bfloat16).astype(np.float64), axis, -1)
    blocks = v.reshape(v.shape[:-1] + (-1, 32))
    amax = np.abs(blocks).max(-1, keepdims=True)
    byte = np.maximum(np.where(amax > 0, np.frexp(amax)[1] - 1 + 127, 0) - down, 1)
    scale = np.exp2(byte - 127.0)
    codes = (blocks / scale).astype(np.float32).astype(dtype).astype(np.float64)
    return np.moveaxis((codes * scale).reshape(v.shape), -1, axis)


WIDE = False


def mx_kscale(k):
    if not WIDE:
        return np.ones(k)
    levels = np.array([10, -10, 5, -5, 0])
    if k % 512:
        return np.exp2(np.random.permutation(np.resize(levels, k // 32))).repeat(32)
    a = np.empty((k // 512, 16))
    for p in range(k // 512):
        a[p, :8] = np.random.permutation(np.resize(levels, 8))
        for g in range(8):
            far = levels[np.abs(levels - a[p, g]) >= 10]
            a[p, g + 8] = far[np.random.randint(len(far))]
    return np.exp2(a.ravel()).repeat(32)


def f64(x):
    return np.asarray(x).astype(np.float64)


def striped(idx):
    return np.tile(idx.reshape(-1, 16).T, (8, 1)).astype(np.uint16)


def unstriped(offs):
    return offs[:16].T.reshape(-1).astype(np.int64)


E2M1 = np.array([0.0, 0.5, 1.0, 1.5, 2.0, 3.0, 4.0, 6.0, -0.0, -0.5, -1.0, -1.5, -2.0, -3.0, -4.0, -6.0])


def pack_weight(w, fmt):
    k, n = w.shape
    w = f64(np.asarray(w, np.float32).astype(ml_dtypes.bfloat16)).reshape(k // 32, 32, n)
    amax = np.abs(w).max(1)
    if fmt == "e4m3":
        byte = np.frexp(amax)[1] - 1 + 127 - 7
    else:
        mant, ex = np.frexp(amax / 6.0)
        byte = np.where(mant > 0.5, ex, ex - 1) + 127
    byte = np.clip(np.where(amax > 0, byte, 1), 1, 254)
    scaled = (w * np.exp2(127.0 - byte)[:, None, :]).reshape(k, n).astype(np.float32)
    by_word = np.ascontiguousarray(scaled.reshape(k // 512, 128, 4, n).transpose(0, 1, 3, 2))
    if fmt == "e4m3":
        words = by_word.astype(ml_dtypes.float8_e4m3fn).view(np.uint8)
    else:
        c = by_word.astype(ml_dtypes.float4_e2m1fn).view(np.uint8) & 0xF
        words = (c[..., 0::2] | (c[..., 1::2] << 4)).reshape(k // 512, 128, 2 * n)
    return np.ascontiguousarray(words), np.ascontiguousarray(byte.astype(np.uint8).reshape(k // 512, 16, n))


def unpack_weight(words, scales, fmt):
    g, _, n = scales.shape
    words = np.ascontiguousarray(words).reshape(g, 128, n, -1)
    if fmt == "e4m3":
        vals = words.view(ml_dtypes.float8_e4m3fn).astype(np.float64)
    else:
        nib = np.empty((g, 128, n, 4), np.uint8)
        nib[..., 0::2] = words & 0xF
        nib[..., 1::2] = words >> 4
        vals = E2M1[nib]
    vals = vals * np.repeat(np.exp2(scales.astype(np.float64) - 127.0), 8, axis=1)[..., None]
    return vals.transpose(0, 1, 3, 2).reshape(g * 512, n)


def gelu(v):
    return 0.5 * v * (1.0 + np.tanh(np.sqrt(2.0 / np.pi) * (v + 0.044715 * v**3)))


K, T, Q, E, C, D, H = 1024, 1024, 768, 4, 256, 256, 0
N = 128


def by_expert(wq, xq, C):
    return np.concatenate([wq[e].T @ xq[:, e * C:(e + 1) * C] for e in range(E)], axis=1)


def setup_inputs():
    n = np.random.standard_normal
    s = mx_kscale(K)
    slot_token = np.random.permutation(T)[:E * C]
    slots2 = np.concatenate([np.random.permutation(Q)[:D] for e in range(E)])
    x = pack_weight(n((K, Q)) * s[:, None], "e4m3")
    return {
        "x_words": x[0],
        "x_scales": x[1],
        "xo": (n((K, T)) * s[:, None]).astype(np.float32),
        "w": (n((E, K, N)) / np.sqrt(K) / s[None, :, None]).astype(np.float32),
        "gate": np.tile(np.random.uniform(0.2, 1.0, E * C), (128, 1)).astype(np.float32),
        "offs": striped(slot_token),
        "offs2": striped(slots2),
    }


def reference(x_words, x_scales, xo, w, gate, offs, offs2):
    wq = mxq(f64(w), 1, "e4m3")
    idx, idx2 = unstriped(offs), unstriped(offs2)
    xq = mxq(f64(xo)[:, idx], 0, "e4m3")
    rq = unpack_weight(x_words, x_scales, "e4m3")[:, idx2]
    y = gelu(by_expert(wq, xq, C))
    z = gelu(by_expert(wq, rq, D))
    own = np.zeros((N, T))
    own[:, idx] = f64(gate[:1]) * y
    return np.concatenate([own, z], axis=1)

@@ -1,0 +1,163 @@
+from contextlib import ExitStack
+
+import concourse.mybir as mybir
+
+K, T, Q, E, C, N = 1024, 1024, 768, 4, 256, 128
+FLOPS = 2 * K * N * 2 * E * C
+
+F32 = mybir.dt.float32
+BF16 = mybir.dt.bfloat16
+I32 = mybir.dt.int32
+U32 = mybir.dt.uint32
+U16 = mybir.dt.uint16
+U8 = mybir.dt.uint8
+FP8X4 = mybir.dt.float8_e4m3fn_x4
+GELU = mybir.ActivationFunctionType.Gelu_apprx_tanh
+MULT = mybir.AluOpType.mult
+
+P = 128
+PACK = 4
+K_PASS = P * PACK
+PASSES = K // K_PASS
+SLOTS = E * C
+HALF = 512
+
+
+def tile_moe_loc_lin_gelu_kernel(tc, x_words, x_scales, xo, w, gate, offs, offs2, out):
+    nc = tc.nc
+    with ExitStack() as ctx:
+        keep = ctx.enter_context(tc.tile_pool(name="keep", bufs=1))
+        psum = ctx.enter_context(tc.psum_pool(name="psum", bufs=1))
+
+        def entries(lst, first, count):
+            return lst[:, first // 16 : (first + count) // 16]
+
+        own_list = keep.tile([P, SLOTS // 16], U16, name="own_list")
+        far_list = keep.tile([P, SLOTS // 16], U16, name="far_list")
+
+        warm_in = keep.tile([P, 8], F32, name="warm_in")
+        warm_out = keep.tile([P, 8], F32, name="warm_out")
+        nc.gpsimd.memset(warm_in[:], 0.0)
+        nc.scalar.activation(warm_out[:], warm_in[:], GELU)
+
+        far_scale_win = keep.tile([P, Q], U8, name="far_scale_win", align_bytes=64)
+        nc.gpsimd.memset(far_scale_win[:].bitcast(I32), 0)
+
+        nc.sync.dma_start(far_list[:], offs2)
+        far_word_win = []
+        for s in range(PASSES):
+            win = keep.tile([P, Q], I32, name=f"far_word_win{s}", align_bytes=64)
+            nc.sync.dma_start(win[:], x_words[s].rearrange("p t d -> p (t d)").bitcast(I32))
+            far_word_win.append(win)
+        for quad in range(4):
+            nc.sync.dma_start(
+                far_scale_win[32 * quad : 32 * quad + 4 * PASSES, :].bitcast(I32),
+                x_scales[:, 4 * quad : 4 * quad + 4, :].bitcast(I32),
+            )
+        nc.sync.dma_start(own_list[:], offs)
+
+        far_codes = []
+        for s in range(PASSES):
+            codes = keep.tile([P, SLOTS], U32, name=f"far_codes{s}", align_bytes=64)
+            for first in range(0, SLOTS, HALF):
+                nc.vector.tensor_copy(
+                    codes[:, first : first + HALF],
+                    far_word_win[s][:].bitcast(U32).indirect(entries(far_list, first, HALF)),
+                )
+            far_codes.append(codes)
+        far_scales = keep.tile([P, SLOTS], U8, name="far_scales", align_bytes=64)
+        for first in range(0, SLOTS, HALF):
+            nc.vector.tensor_copy(
+                far_scales[:, first : first + HALF], far_scale_win[:].indirect(entries(far_list, first, HALF))
+            )
+
+        picked = keep.tile([P, PASSES, 2, 2 * SLOTS], BF16, name="picked", align_bytes=64)
+
+        def gather_own(s, u, cut):
+            rows = xo[s * K_PASS : (s + 1) * K_PASS, :].rearrange("(p j) t -> p j t", j=PACK)
+            pairs = keep.tile([P, T, 2], BF16, name=f"pairs{s}{u}", align_bytes=64)
+            for h in range(T // HALF):
+                raw = keep.tile([P, 2, HALF], F32, name=f"raw{s}{u}{h}")
+                nc.sync.dma_start(raw[:], rows[:, 2 * u : 2 * u + 2, h * HALF : (h + 1) * HALF])
+                nc.scalar.copy(pairs[:, h * HALF : (h + 1) * HALF, :], raw[:].rearrange("p j t -> p t j"))
+            for first in range(0, SLOTS, cut):
+                nc.vector.tensor_copy(
+                    picked[:, s, u, 2 * first : 2 * (first + cut)].bitcast(U32),
+                    pairs[:].rearrange("p t j -> p (t j)").bitcast(U32).indirect(entries(own_list, first, cut)),
+                )
+
+        def quantise_weights(e):
+            w_raw = keep.tile([P, PASSES, PACK, N], F32, name=f"w_raw{e}")
+            nc.sync.dma_start(w_raw[:], w[e].rearrange("(s p j) n -> p s j n", s=PASSES, j=PACK))
+            w_bf = keep.tile([P, PASSES, N, PACK], BF16, name=f"w_bf{e}", align_bytes=64)
+            nc.scalar.copy(w_bf[:], w_raw[:].rearrange("p s j n -> p s n j"))
+            w_codes = keep.tile([P, PASSES * N], U32, name=f"w_codes{e}", align_bytes=64)
+            w_scales = keep.tile([P, PASSES * N], U8, name=f"w_scales{e}", align_bytes=64)
+            nc.vector.quantize_mx(
+                out=w_codes[:].bitcast(FP8X4), scales=w_scales[:], in_=w_bf[:].rearrange("p s n j -> p (s n j)")
+            )
+            return w_codes, w_scales
+
+        weights = []
+        gather_own(0, 0, HALF)
+        weights.append(quantise_weights(0))
+        gather_own(0, 1, HALF)
+        weights.append(quantise_weights(1))
+        gather_own(1, 0, HALF)
+        weights.append(quantise_weights(2))
+        gather_own(1, 1, C)
+        weights.append(quantise_weights(3))
+        gate_sb = keep.tile([P, SLOTS], F32, name="gate_sb")
+        nc.sync.dma_start(gate_sb[:], gate)
+
+        own_out = keep.tile([P, T], F32, name="own_out")
+
+        def product(acc, e, codes, scales):
+            w_codes, w_scales = weights[e]
+            for s in range(PASSES):
+                nc.tensor.matmul_mx(
+                    out=acc,
+                    lhsT=w_codes[:, s * N : (s + 1) * N].bitcast(FP8X4),
+                    lhsT_scale=w_scales[:, s * N : (s + 1) * N],
+                    rhs=codes(s).bitcast(FP8X4),
+                    rhs_scale=scales(s),
+                    start=(s == 0),
+                    stop=(s == PASSES - 1),
+                )
+
+        def multiply(e):
+            cols = slice(e * C, (e + 1) * C)
+            x_bf = keep.tile([P, PASSES, C * PACK], BF16, name=f"x_bf{e}", align_bytes=64)
+            nc.scalar.copy(
+                x_bf[:].bitcast(F32).rearrange("p s (c u) -> p s c u", u=2),
+                picked[:].bitcast(F32)[:, :, :, cols].rearrange("p s u c -> p s c u"),
+            )
+            x_codes = keep.tile([P, PASSES * C], U32, name=f"x_codes{e}", align_bytes=64)
+            x_planes = keep.tile([P, PASSES * C], U8, name=f"x_planes{e}", align_bytes=64)
+            nc.vector.quantize_mx(
+                out=x_codes[:].bitcast(FP8X4), scales=x_planes[:], in_=x_bf[:].rearrange("p s c -> p (s c)")
+            )
+            acc = psum.tile([N, 2, C], F32, name=f"acc{e}")
+            product(acc[:, 1, :], e, lambda s: far_codes[s][:, cols], lambda s: far_scales[4 * s : P, cols])
+            product(
+                acc[:, 0, :], e,
+                lambda s: x_codes[:, s * C : (s + 1) * C], lambda s: x_planes[:, s * C : (s + 1) * C],
+            )
+            return acc
+
+        def finish(e, acc):
+            act = keep.tile([N, 2, C], F32, name=f"act{e}")
+            nc.scalar.activation(act[:], acc[:], GELU)
+            nc.sync.dma_start(out[:, T + e * C : T + (e + 1) * C], act[:, 1, :])
+            nc.vector.tensor_tensor(
+                own_out[:].indirect(entries(own_list, e * C, C)), act[:, 0, :], gate_sb[:, e * C : (e + 1) * C], MULT
+            )
+
+        LAG = 2
+        sums = []
+        for step in range(E + LAG):
+            if step < E:
+                sums.append(multiply(step))
+            if step >= LAG:
+                finish(step - LAG, sums[step - LAG])
+        nc.sync.dma_start(out[:, 0:T], own_out[:])

@@ -13,7 +13,9 @@ U16 = mybir.dt.uint16
 U8 = mybir.dt.uint8
 FP8X4 = mybir.dt.float8_e4m3fn_x4
 GELU = mybir.ActivationFunctionType.Gelu_apprx_tanh
+COPY = mybir.ActivationFunctionType.Copy
 MULT = mybir.AluOpType.mult
+ADD = mybir.AluOpType.add
 
 P = 128
 PACK = 4
@@ -37,11 +39,11 @@ def tile_moe_loc_lin_gelu_kernel(tc, x_words, x_scales, xo, w, gate, offs, offs2
 
         warm_in = keep.tile([P, 8], F32, name="warm_in")
         warm_out = keep.tile([P, 8], F32, name="warm_out")
-        nc.gpsimd.memset(warm_in[:], 0.0)
+        nc.vector.memset(warm_in[:], 0.0)
         nc.scalar.activation(warm_out[:], warm_in[:], GELU)
 
         far_scale_win = keep.tile([P, Q], U8, name="far_scale_win", align_bytes=64)
-        nc.gpsimd.memset(far_scale_win[:].bitcast(I32), 0)
+        nc.vector.memset(far_scale_win[:].bitcast(I32), 0)
 
         nc.sync.dma_start(far_list[:], offs2)
         far_word_win = []
@@ -73,24 +75,50 @@ def tile_moe_loc_lin_gelu_kernel(tc, x_words, x_scales, xo, w, gate, offs, offs2
 
         picked = keep.tile([P, PASSES, 2, 2 * SLOTS], BF16, name="picked", align_bytes=64)
 
-        def gather_own(s, u, cut):
-            rows = xo[s * K_PASS : (s + 1) * K_PASS, :].rearrange("(p j) t -> p j t", j=PACK)
+        def round_on_scalar(dst, src):
+            nc.scalar.copy(dst, src)
+
+        def round_on_gpsimd(dst, src):
+            nc.gpsimd.tensor_scalar(dst, src, 1.0, 0.0, MULT, ADD)
+
+        def pass_rows(s):
+            return xo[s * K_PASS : (s + 1) * K_PASS, :].rearrange("(p j) t -> p j t", j=PACK)
+
+        def round_pairs(s, u, rounders):
             pairs = keep.tile([P, T, 2], BF16, name=f"pairs{s}{u}", align_bytes=64)
             for h in range(T // HALF):
                 raw = keep.tile([P, 2, HALF], F32, name=f"raw{s}{u}{h}")
-                nc.sync.dma_start(raw[:], rows[:, 2 * u : 2 * u + 2, h * HALF : (h + 1) * HALF])
-                nc.scalar.copy(pairs[:, h * HALF : (h + 1) * HALF, :], raw[:].rearrange("p j t -> p t j"))
+                nc.sync.dma_start(raw[:], pass_rows(s)[:, 2 * u : 2 * u + 2, h * HALF : (h + 1) * HALF])
+                rounders[h](pairs[:, h * HALF : (h + 1) * HALF, :], raw[:].rearrange("p j t -> p t j"))
+            return pairs
+
+        def gather_pairs(s, u, pairs, cut):
             for first in range(0, SLOTS, cut):
                 nc.vector.tensor_copy(
                     picked[:, s, u, 2 * first : 2 * (first + cut)].bitcast(U32),
                     pairs[:].rearrange("p t j -> p (t j)").bitcast(U32).indirect(entries(own_list, first, cut)),
                 )
 
+        def round_row(s, j):
+            raw = keep.tile([P, T], F32, name=f"raw_row{s}{j}")
+            nc.sync.dma_start(raw[:], pass_rows(s)[:, j, :])
+            row = keep.tile([P, T], BF16, name=f"row{s}{j}", align_bytes=64)
+            round_on_gpsimd(row[:], raw[:])
+            return row
+
+        def gather_row(s, j, row):
+            for first in range(0, SLOTS, HALF):
+                nc.scalar.activation(
+                    picked[:, s, j // 2, 2 * first + j % 2 : 2 * (first + HALF) : 2],
+                    row[:].indirect(entries(own_list, first, HALF)),
+                    COPY,
+                )
+
         def quantise_weights(e):
             w_raw = keep.tile([P, PASSES, PACK, N], F32, name=f"w_raw{e}")
             nc.sync.dma_start(w_raw[:], w[e].rearrange("(s p j) n -> p s j n", s=PASSES, j=PACK))
             w_bf = keep.tile([P, PASSES, N, PACK], BF16, name=f"w_bf{e}", align_bytes=64)
-            nc.scalar.copy(w_bf[:], w_raw[:].rearrange("p s j n -> p s n j"))
+            round_on_gpsimd(w_bf[:], w_raw[:].rearrange("p s j n -> p s n j"))
             w_codes = keep.tile([P, PASSES * N], U32, name=f"w_codes{e}", align_bytes=64)
             w_scales = keep.tile([P, PASSES * N], U8, name=f"w_scales{e}", align_bytes=64)
             nc.vector.quantize_mx(
@@ -98,15 +126,14 @@ def tile_moe_loc_lin_gelu_kernel(tc, x_words, x_scales, xo, w, gate, offs, offs2
             )
             return w_codes, w_scales
 
-        weights = []
-        gather_own(0, 0, HALF)
-        weights.append(quantise_weights(0))
-        gather_own(0, 1, HALF)
-        weights.append(quantise_weights(1))
-        gather_own(1, 0, HALF)
-        weights.append(quantise_weights(2))
-        gather_own(1, 1, C)
-        weights.append(quantise_weights(3))
+        gather_pairs(0, 0, round_pairs(0, 0, (round_on_scalar, round_on_scalar)), HALF)
+        row2 = round_row(0, 2)
+        gather_pairs(1, 0, round_pairs(1, 0, (round_on_scalar, round_on_gpsimd)), HALF)
+        row3 = round_row(0, 3)
+        gather_pairs(1, 1, round_pairs(1, 1, (round_on_scalar, round_on_gpsimd)), C)
+        gather_row(0, 2, row2)
+        gather_row(0, 3, row3)
+        weights = [quantise_weights(e) for e in range(E)]
         gate_sb = keep.tile([P, SLOTS], F32, name="gate_sb")
         nc.sync.dma_start(gate_sb[:], gate)
 

@@ -46,18 +46,23 @@ def tile_moe_loc_lin_gelu_kernel(tc, x_words, x_scales, xo, w, gate, offs, offs2
         nc.vector.memset(far_scale_win[:].bitcast(I32), 0)
 
         nc.sync.dma_start(far_list[:], offs2)
-        far_word_win = []
-        for s in range(PASSES):
-            win = keep.tile([P, Q], I32, name=f"far_word_win{s}", align_bytes=64)
-            nc.sync.dma_start(win[:], x_words[s].rearrange("p t d -> p (t d)").bitcast(I32))
-            far_word_win.append(win)
         for quad in range(4):
             nc.sync.dma_start(
                 far_scale_win[32 * quad : 32 * quad + 4 * PASSES, :].bitcast(I32),
                 x_scales[:, 4 * quad : 4 * quad + 4, :].bitcast(I32),
             )
+        far_word_win = []
+        for s in range(PASSES):
+            win = keep.tile([P, Q], I32, name=f"far_word_win{s}", align_bytes=64)
+            nc.sync.dma_start(win[:], x_words[s].rearrange("p t d -> p (t d)").bitcast(I32))
+            far_word_win.append(win)
         nc.sync.dma_start(own_list[:], offs)
 
+        far_scales = keep.tile([P, SLOTS], U8, name="far_scales", align_bytes=64)
+        for first in range(0, SLOTS, HALF):
+            nc.vector.tensor_copy(
+                far_scales[:, first : first + HALF], far_scale_win[:].indirect(entries(far_list, first, HALF))
+            )
         far_codes = []
         for s in range(PASSES):
             codes = keep.tile([P, SLOTS], U32, name=f"far_codes{s}", align_bytes=64)
@@ -67,11 +72,6 @@ def tile_moe_loc_lin_gelu_kernel(tc, x_words, x_scales, xo, w, gate, offs, offs2
                     far_word_win[s][:].bitcast(U32).indirect(entries(far_list, first, HALF)),
                 )
             far_codes.append(codes)
-        far_scales = keep.tile([P, SLOTS], U8, name="far_scales", align_bytes=64)
-        for first in range(0, SLOTS, HALF):
-            nc.vector.tensor_copy(
-                far_scales[:, first : first + HALF], far_scale_win[:].indirect(entries(far_list, first, HALF))
-            )
 
         picked = keep.tile([P, PASSES, 2, 2 * SLOTS], BF16, name="picked", align_bytes=64)
 
@@ -84,13 +84,10 @@ def tile_moe_loc_lin_gelu_kernel(tc, x_words, x_scales, xo, w, gate, offs, offs2
         def pass_rows(s):
             return xo[s * K_PASS : (s + 1) * K_PASS, :].rearrange("(p j) t -> p j t", j=PACK)
 
-        def round_pairs(s, u, rounders):
-            pairs = keep.tile([P, T, 2], BF16, name=f"pairs{s}{u}", align_bytes=64)
-            for h in range(T // HALF):
-                raw = keep.tile([P, 2, HALF], F32, name=f"raw{s}{u}{h}")
-                nc.sync.dma_start(raw[:], pass_rows(s)[:, 2 * u : 2 * u + 2, h * HALF : (h + 1) * HALF])
-                rounders[h](pairs[:, h * HALF : (h + 1) * HALF, :], raw[:].rearrange("p j t -> p t j"))
-            return pairs
+        def round_pairs(pairs, s, u, h, rounder):
+            raw = keep.tile([P, 2, HALF], F32, name=f"raw{s}{u}{h}")
+            nc.sync.dma_start(raw[:], pass_rows(s)[:, 2 * u : 2 * u + 2, h * HALF : (h + 1) * HALF])
+            rounder(pairs[:, h * HALF : (h + 1) * HALF, :], raw[:].rearrange("p j t -> p t j"))
 
         def gather_pairs(s, u, pairs, cut):
             for first in range(0, SLOTS, cut):
@@ -103,7 +100,7 @@ def tile_moe_loc_lin_gelu_kernel(tc, x_words, x_scales, xo, w, gate, offs, offs2
             raw = keep.tile([P, T], F32, name=f"raw_row{s}{j}")
             nc.sync.dma_start(raw[:], pass_rows(s)[:, j, :])
             row = keep.tile([P, T], BF16, name=f"row{s}{j}", align_bytes=64)
-            round_on_gpsimd(row[:], raw[:])
+            round_on_scalar(row[:], raw[:])
             return row
 
         def gather_row(s, j, row):
@@ -114,11 +111,21 @@ def tile_moe_loc_lin_gelu_kernel(tc, x_words, x_scales, xo, w, gate, offs, offs2
                     COPY,
                 )
 
-        def quantise_weights(e):
+        def load_weights(e):
             w_raw = keep.tile([P, PASSES, PACK, N], F32, name=f"w_raw{e}")
             nc.sync.dma_start(w_raw[:], w[e].rearrange("(s p j) n -> p s j n", s=PASSES, j=PACK))
+            return w_raw
+
+        def quantise_weights(e, w_raw, rounder):
             w_bf = keep.tile([P, PASSES, N, PACK], BF16, name=f"w_bf{e}", align_bytes=64)
-            round_on_gpsimd(w_bf[:], w_raw[:].rearrange("p s j n -> p s n j"))
+            if rounder is round_on_gpsimd:
+                rounder(w_bf[:], w_raw[:].rearrange("p s j n -> p s n j"))
+            else:
+                for s in range(PASSES):
+                    rounder(
+                        w_bf[:, s, :, :].rearrange("p (c i) j -> p c j i", i=4),
+                        w_raw[:, s, :, :].rearrange("p j (c i) -> p c j i", i=4),
+                    )
             w_codes = keep.tile([P, PASSES * N], U32, name=f"w_codes{e}", align_bytes=64)
             w_scales = keep.tile([P, PASSES * N], U8, name=f"w_scales{e}", align_bytes=64)
             nc.vector.quantize_mx(
@@ -126,16 +133,27 @@ def tile_moe_loc_lin_gelu_kernel(tc, x_words, x_scales, xo, w, gate, offs, offs2
             )
             return w_codes, w_scales
 
-        gather_pairs(0, 0, round_pairs(0, 0, (round_on_scalar, round_on_scalar)), HALF)
+        pairs = [
+            keep.tile([P, T, 2], BF16, name=f"pairs{i}", align_bytes=64) for i in range(3)
+        ]
+        round_pairs(pairs[0], 0, 0, 0, round_on_scalar)
+        round_pairs(pairs[0], 0, 0, 1, round_on_scalar)
+        gather_pairs(0, 0, pairs[0], HALF)
         row2 = round_row(0, 2)
-        gather_pairs(1, 0, round_pairs(1, 0, (round_on_scalar, round_on_gpsimd)), HALF)
+        round_pairs(pairs[1], 1, 0, 0, round_on_gpsimd)
+        round_pairs(pairs[1], 1, 0, 1, round_on_gpsimd)
+        gather_pairs(1, 0, pairs[1], HALF)
+        round_pairs(pairs[2], 1, 1, 0, round_on_gpsimd)
         row3 = round_row(0, 3)
-        gather_pairs(1, 1, round_pairs(1, 1, (round_on_scalar, round_on_gpsimd)), C)
+        round_pairs(pairs[2], 1, 1, 1, round_on_gpsimd)
+        gather_pairs(1, 1, pairs[2], C)
         gather_row(0, 2, row2)
         gather_row(0, 3, row3)
-        weights = [quantise_weights(e) for e in range(E)]
+        w_raws = [load_weights(0), load_weights(1)]
         gate_sb = keep.tile([P, SLOTS], F32, name="gate_sb")
         nc.sync.dma_start(gate_sb[:], gate)
+        w_raws += [load_weights(2), load_weights(3)]
+        weights = []
 
         own_out = keep.tile([P, T], F32, name="own_out")
 
@@ -154,6 +172,7 @@ def tile_moe_loc_lin_gelu_kernel(tc, x_words, x_scales, xo, w, gate, offs, offs2
 
         def multiply(e):
             cols = slice(e * C, (e + 1) * C)
+            weights.append(quantise_weights(e, w_raws[e], round_on_gpsimd if e < 2 else round_on_scalar))
             x_bf = keep.tile([P, PASSES, C * PACK], BF16, name=f"x_bf{e}", align_bytes=64)
             nc.scalar.copy(
                 x_bf[:].bitcast(F32).rearrange("p s (c u) -> p s c u", u=2),
@@ -180,7 +199,7 @@ def tile_moe_loc_lin_gelu_kernel(tc, x_words, x_scales, xo, w, gate, offs, offs2
                 own_out[:].indirect(entries(own_list, e * C, C)), act[:, 0, :], gate_sb[:, e * C : (e + 1) * C], MULT
             )
 
-        LAG = 2
+        LAG = 1
         sums = []
         for step in range(E + LAG):
             if step < E:

@@ -46,23 +46,20 @@ def tile_moe_loc_lin_gelu_kernel(tc, x_words, x_scales, xo, w, gate, offs, offs2
         nc.vector.memset(far_scale_win[:].bitcast(I32), 0)
 
         nc.sync.dma_start(far_list[:], offs2)
-        for quad in range(4):
-            nc.sync.dma_start(
-                far_scale_win[32 * quad : 32 * quad + 4 * PASSES, :].bitcast(I32),
-                x_scales[:, 4 * quad : 4 * quad + 4, :].bitcast(I32),
-            )
         far_word_win = []
         for s in range(PASSES):
             win = keep.tile([P, Q], I32, name=f"far_word_win{s}", align_bytes=64)
             nc.sync.dma_start(win[:], x_words[s].rearrange("p t d -> p (t d)").bitcast(I32))
             far_word_win.append(win)
+            if s == 0:
+                for quad in range(4):
+                    nc.sync.dma_start(
+                        far_scale_win[32 * quad : 32 * quad + 4 * PASSES, :].bitcast(I32),
+                        x_scales[:, 4 * quad : 4 * quad + 4, :].bitcast(I32),
+                    )
         nc.sync.dma_start(own_list[:], offs)
 
         far_scales = keep.tile([P, SLOTS], U8, name="far_scales", align_bytes=64)
-        for first in range(0, SLOTS, HALF):
-            nc.vector.tensor_copy(
-                far_scales[:, first : first + HALF], far_scale_win[:].indirect(entries(far_list, first, HALF))
-            )
         far_codes = []
         for s in range(PASSES):
             codes = keep.tile([P, SLOTS], U32, name=f"far_codes{s}", align_bytes=64)
@@ -72,6 +69,11 @@ def tile_moe_loc_lin_gelu_kernel(tc, x_words, x_scales, xo, w, gate, offs, offs2
                     far_word_win[s][:].bitcast(U32).indirect(entries(far_list, first, HALF)),
                 )
             far_codes.append(codes)
+            if s == 0:
+                for first in range(0, SLOTS, HALF):
+                    nc.vector.tensor_copy(
+                        far_scales[:, first : first + HALF], far_scale_win[:].indirect(entries(far_list, first, HALF))
+                    )
 
         picked = keep.tile([P, PASSES, 2, 2 * SLOTS], BF16, name="picked", align_bytes=64)
 
@@ -84,10 +86,17 @@ def tile_moe_loc_lin_gelu_kernel(tc, x_words, x_scales, xo, w, gate, offs, offs2
         def pass_rows(s):
             return xo[s * K_PASS : (s + 1) * K_PASS, :].rearrange("(p j) t -> p j t", j=PACK)
 
-        def round_pairs(pairs, s, u, h, rounder):
-            raw = keep.tile([P, 2, HALF], F32, name=f"raw{s}{u}{h}")
-            nc.sync.dma_start(raw[:], pass_rows(s)[:, 2 * u : 2 * u + 2, h * HALF : (h + 1) * HALF])
-            rounder(pairs[:, h * HALF : (h + 1) * HALF, :], raw[:].rearrange("p j t -> p t j"))
+        def round_pairs(pairs, s, u, first, shares):
+            width = sum(count for count, rounder in shares)
+            raw = keep.tile([P, 2, width], F32, name=f"raw{s}{u}_{first}")
+            nc.sync.dma_start(raw[:], pass_rows(s)[:, 2 * u : 2 * u + 2, first : first + width])
+            done = 0
+            for count, rounder in shares:
+                rounder(
+                    pairs[:, first + done : first + done + count, :],
+                    raw[:, :, done : done + count].rearrange("p j t -> p t j"),
+                )
+                done += count
 
         def gather_pairs(s, u, pairs, cut):
             for first in range(0, SLOTS, cut):
@@ -136,23 +145,22 @@ def tile_moe_loc_lin_gelu_kernel(tc, x_words, x_scales, xo, w, gate, offs, offs2
         pairs = [
             keep.tile([P, T, 2], BF16, name=f"pairs{i}", align_bytes=64) for i in range(3)
         ]
-        round_pairs(pairs[0], 0, 0, 0, round_on_scalar)
-        round_pairs(pairs[0], 0, 0, 1, round_on_scalar)
+        round_pairs(pairs[0], 0, 0, 0, [(HALF, round_on_scalar), (HALF, round_on_gpsimd)])
         gather_pairs(0, 0, pairs[0], HALF)
         row2 = round_row(0, 2)
-        round_pairs(pairs[1], 1, 0, 0, round_on_gpsimd)
-        round_pairs(pairs[1], 1, 0, 1, round_on_gpsimd)
+        round_pairs(pairs[1], 1, 0, 0, [(HALF, round_on_scalar), (HALF, round_on_gpsimd)])
         gather_pairs(1, 0, pairs[1], HALF)
-        round_pairs(pairs[2], 1, 1, 0, round_on_gpsimd)
+        round_pairs(pairs[2], 1, 1, 0, [(HALF, round_on_gpsimd)])
         row3 = round_row(0, 3)
-        round_pairs(pairs[2], 1, 1, 1, round_on_gpsimd)
+        round_pairs(pairs[2], 1, 1, HALF, [(C, round_on_gpsimd)])
+        round_pairs(pairs[2], 1, 1, HALF + C, [(C, round_on_gpsimd)])
         gather_pairs(1, 1, pairs[2], C)
         gather_row(0, 2, row2)
         gather_row(0, 3, row3)
-        w_raws = [load_weights(0), load_weights(1)]
+        w_raws = [load_weights(0), load_weights(1), load_weights(2)]
         gate_sb = keep.tile([P, SLOTS], F32, name="gate_sb")
         nc.sync.dma_start(gate_sb[:], gate)
-        w_raws += [load_weights(2), load_weights(3)]
+        w_raws.append(load_weights(3))
         weights = []
 
         own_out = keep.tile([P, T], F32, name="own_out")
@@ -183,20 +191,18 @@ def tile_moe_loc_lin_gelu_kernel(tc, x_words, x_scales, xo, w, gate, offs, offs2
             nc.vector.quantize_mx(
                 out=x_codes[:].bitcast(FP8X4), scales=x_planes[:], in_=x_bf[:].rearrange("p s c -> p (s c)")
             )
-            acc = psum.tile([N, 2, C], F32, name=f"acc{e}")
-            product(acc[:, 1, :], e, lambda s: far_codes[s][:, cols], lambda s: far_scales[4 * s : P, cols])
+            acc = psum.tile([N, C], F32, name=f"own_acc{e}")
             product(
-                acc[:, 0, :], e,
+                acc[:], e,
                 lambda s: x_codes[:, s * C : (s + 1) * C], lambda s: x_planes[:, s * C : (s + 1) * C],
             )
             return acc
 
         def finish(e, acc):
-            act = keep.tile([N, 2, C], F32, name=f"act{e}")
+            act = keep.tile([N, C], F32, name=f"act{e}")
             nc.scalar.activation(act[:], acc[:], GELU)
-            nc.sync.dma_start(out[:, T + e * C : T + (e + 1) * C], act[:, 1, :])
             nc.vector.tensor_tensor(
-                own_out[:].indirect(entries(own_list, e * C, C)), act[:, 0, :], gate_sb[:, e * C : (e + 1) * C], MULT
+                own_out[:].indirect(entries(own_list, e * C, C)), act[:], gate_sb[:, e * C : (e + 1) * C], MULT
             )
 
         LAG = 1
@@ -206,4 +212,16 @@ def tile_moe_loc_lin_gelu_kernel(tc, x_words, x_scales, xo, w, gate, offs, offs2
                 sums.append(multiply(step))
             if step >= LAG:
                 finish(step - LAG, sums[step - LAG])
+
+        for first in range(0, E, 2):
+            far_acc = psum.tile([N, 2, C], F32, name=f"far_acc{first}")
+            for i in range(2):
+                cols = slice((first + i) * C, (first + i + 1) * C)
+                product(
+                    far_acc[:, i, :], first + i,
+                    lambda s: far_codes[s][:, cols], lambda s: far_scales[4 * s : P, cols],
+                )
+            far_act = keep.tile([N, 2 * C], F32, name=f"far_act{first}")
+            nc.scalar.activation(far_act[:], far_acc[:].rearrange("p i c -> p (i c)"), GELU)
+            nc.scalar.dma_start(out[:, T + first * C : T + (first + 2) * C], far_act[:])
         nc.sync.dma_start(out[:, 0:T], own_out[:])

@@ -29,6 +29,7 @@ def tile_moe_loc_lin_gelu_kernel(tc, x_words, x_scales, xo, w, gate, offs, offs2
     nc = tc.nc
     with ExitStack() as ctx:
         keep = ctx.enter_context(tc.tile_pool(name="keep", bufs=1))
+        reuse = ctx.enter_context(tc.tile_pool(name="reuse", bufs=1))
         psum = ctx.enter_context(tc.psum_pool(name="psum", bufs=1))
 
         def entries(lst, first, count):
@@ -45,37 +46,18 @@ def tile_moe_loc_lin_gelu_kernel(tc, x_words, x_scales, xo, w, gate, offs, offs2
         far_scale_win = keep.tile([P, Q], U8, name="far_scale_win", align_bytes=64)
         nc.vector.memset(far_scale_win[:].bitcast(I32), 0)
 
-        nc.sync.dma_start(far_list[:], offs2)
-        far_word_win = []
-        for s in range(PASSES):
+        def load_far_words(s):
             win = keep.tile([P, Q], I32, name=f"far_word_win{s}", align_bytes=64)
             nc.sync.dma_start(win[:], x_words[s].rearrange("p t d -> p (t d)").bitcast(I32))
-            far_word_win.append(win)
-            if s == 0:
-                for quad in range(4):
-                    nc.sync.dma_start(
-                        far_scale_win[32 * quad : 32 * quad + 4 * PASSES, :].bitcast(I32),
-                        x_scales[:, 4 * quad : 4 * quad + 4, :].bitcast(I32),
-                    )
-        nc.sync.dma_start(own_list[:], offs)
+            return win
 
-        far_scales = keep.tile([P, SLOTS], U8, name="far_scales", align_bytes=64)
-        far_codes = []
-        for s in range(PASSES):
+        def gather_far_words(s, win):
             codes = keep.tile([P, SLOTS], U32, name=f"far_codes{s}", align_bytes=64)
             for first in range(0, SLOTS, HALF):
                 nc.vector.tensor_copy(
-                    codes[:, first : first + HALF],
-                    far_word_win[s][:].bitcast(U32).indirect(entries(far_list, first, HALF)),
+                    codes[:, first : first + HALF], win[:].bitcast(U32).indirect(entries(far_list, first, HALF))
                 )
-            far_codes.append(codes)
-            if s == 0:
-                for first in range(0, SLOTS, HALF):
-                    nc.vector.tensor_copy(
-                        far_scales[:, first : first + HALF], far_scale_win[:].indirect(entries(far_list, first, HALF))
-                    )
-
-        picked = keep.tile([P, PASSES, 2, 2 * SLOTS], BF16, name="picked", align_bytes=64)
+            return codes
 
         def round_on_scalar(dst, src):
             nc.scalar.copy(dst, src)
@@ -86,9 +68,15 @@ def tile_moe_loc_lin_gelu_kernel(tc, x_words, x_scales, xo, w, gate, offs, offs2
         def pass_rows(s):
             return xo[s * K_PASS : (s + 1) * K_PASS, :].rearrange("(p j) t -> p j t", j=PACK)
 
-        def round_pairs(pairs, s, u, first, shares):
+        picked = [
+            [keep.tile([P, 2, 2 * HALF], BF16, name=f"picked{s}{h}", align_bytes=64) for h in range(2)]
+            for s in range(PASSES)
+        ]
+
+        def round_pairs(pairs, s, u, first, shares, raw=None):
             width = sum(count for count, rounder in shares)
-            raw = keep.tile([P, 2, width], F32, name=f"raw{s}{u}_{first}")
+            if raw is None:
+                raw = keep.tile([P, 2, width], F32, name=f"raw{s}{u}_{first}")
             nc.sync.dma_start(raw[:], pass_rows(s)[:, 2 * u : 2 * u + 2, first : first + width])
             done = 0
             for count, rounder in shares:
@@ -98,35 +86,52 @@ def tile_moe_loc_lin_gelu_kernel(tc, x_words, x_scales, xo, w, gate, offs, offs2
                 )
                 done += count
 
-        def gather_pairs(s, u, pairs, cut):
-            for first in range(0, SLOTS, cut):
+        def gather_pairs(s, u, pairs):
+            for h in range(2):
                 nc.vector.tensor_copy(
-                    picked[:, s, u, 2 * first : 2 * (first + cut)].bitcast(U32),
-                    pairs[:].rearrange("p t j -> p (t j)").bitcast(U32).indirect(entries(own_list, first, cut)),
+                    picked[s][h][:, u, :].bitcast(U32),
+                    pairs[:].rearrange("p t j -> p (t j)").bitcast(U32).indirect(entries(own_list, h * HALF, HALF)),
                 )
 
-        def round_row(s, j):
+        def round_row(s, j, shares):
             raw = keep.tile([P, T], F32, name=f"raw_row{s}{j}")
             nc.sync.dma_start(raw[:], pass_rows(s)[:, j, :])
             row = keep.tile([P, T], BF16, name=f"row{s}{j}", align_bytes=64)
-            round_on_scalar(row[:], raw[:])
+            done = 0
+            for count, rounder in shares:
+                rounder(row[:, done : done + count], raw[:, done : done + count])
+                done += count
             return row
 
         def gather_row(s, j, row):
-            for first in range(0, SLOTS, HALF):
+            for h in range(2):
                 nc.scalar.activation(
-                    picked[:, s, j // 2, 2 * first + j % 2 : 2 * (first + HALF) : 2],
-                    row[:].indirect(entries(own_list, first, HALF)),
+                    picked[s][h][:, j // 2, j % 2 : 2 * HALF : 2],
+                    row[:].indirect(entries(own_list, h * HALF, HALF)),
                     COPY,
                 )
 
+        x_bf = [keep.tile([P, PASSES, C * PACK], BF16, name=f"x_bf{e}", align_bytes=64) for e in range(2)]
+        x_bf += [
+            reuse.tile([P, PASSES, C * PACK], BF16, name=f"x_bf{e}", align_bytes=64, offset=(e - 2) * 4096)
+            for e in range(2, E)
+        ]
+        last_raw = reuse.tile([P, 2, HALF], F32, name="last_raw", align_bytes=64, offset=2048)
+
+        def weave(s, e):
+            cols = slice(e % 2 * C, (e % 2 + 1) * C)
+            nc.scalar.copy(
+                x_bf[e][:, s, :].bitcast(F32).rearrange("p (c u) -> p c u", u=2),
+                picked[s][e // 2][:].bitcast(F32)[:, :, cols].rearrange("p u c -> p c u"),
+            )
+
         def load_weights(e):
-            w_raw = keep.tile([P, PASSES, PACK, N], F32, name=f"w_raw{e}")
+            w_raw = keep.tile([P, PASSES, PACK, N], F32, name=f"w_raw{e}", tag=f"w_raw{e}")
             nc.sync.dma_start(w_raw[:], w[e].rearrange("(s p j) n -> p s j n", s=PASSES, j=PACK))
             return w_raw
 
         def quantise_weights(e, w_raw, rounder):
-            w_bf = keep.tile([P, PASSES, N, PACK], BF16, name=f"w_bf{e}", align_bytes=64)
+            w_bf = keep.tile([P, PASSES, N, PACK], BF16, name=f"w_bf{e}", tag=f"w_bf{e}", align_bytes=64)
             if rounder is round_on_gpsimd:
                 rounder(w_bf[:], w_raw[:].rearrange("p s j n -> p s n j"))
             else:
@@ -142,25 +147,42 @@ def tile_moe_loc_lin_gelu_kernel(tc, x_words, x_scales, xo, w, gate, offs, offs2
             )
             return w_codes, w_scales
 
-        pairs = [
-            keep.tile([P, T, 2], BF16, name=f"pairs{i}", align_bytes=64) for i in range(3)
-        ]
-        round_pairs(pairs[0], 0, 0, 0, [(HALF, round_on_scalar), (HALF, round_on_gpsimd)])
-        gather_pairs(0, 0, pairs[0], HALF)
-        row2 = round_row(0, 2)
-        round_pairs(pairs[1], 1, 0, 0, [(HALF, round_on_scalar), (HALF, round_on_gpsimd)])
-        gather_pairs(1, 0, pairs[1], HALF)
+        nc.sync.dma_start(far_list[:], offs2)
+        win0 = load_far_words(0)
+        for quad in range(4):
+            nc.sync.dma_start(
+                far_scale_win[32 * quad : 32 * quad + 4 * PASSES, :].bitcast(I32),
+                x_scales[:, 4 * quad : 4 * quad + 4, :].bitcast(I32),
+            )
+        nc.sync.dma_start(own_list[:], offs)
+        far_codes = [gather_far_words(0, win0)]
+        far_scales = keep.tile([P, SLOTS], U8, name="far_scales", align_bytes=64)
+        for first in range(0, SLOTS, HALF):
+            nc.vector.tensor_copy(
+                far_scales[:, first : first + HALF], far_scale_win[:].indirect(entries(far_list, first, HALF))
+            )
+
+        pairs = [keep.tile([P, T, 2], BF16, name=f"pairs{i}", align_bytes=64) for i in range(3)]
+        gather_row(0, 2, round_row(0, 2, [(HALF, round_on_scalar), (HALF, round_on_gpsimd)]))
+        gather_row(0, 3, round_row(0, 3, [(T, round_on_gpsimd)]))
+        round_pairs(pairs[0], 0, 0, 0, [(HALF, round_on_gpsimd)])
+        far_codes.append(gather_far_words(1, load_far_words(1)))
+        round_pairs(pairs[0], 0, 0, HALF, [(HALF, round_on_gpsimd)])
+        gather_pairs(0, 0, pairs[0])
+        round_pairs(pairs[1], 1, 0, 0, [(HALF, round_on_gpsimd)])
+        round_pairs(pairs[1], 1, 0, HALF, [(HALF, round_on_gpsimd)])
+        gather_pairs(1, 0, pairs[1])
+        weave(0, 0)
+        weave(0, 1)
         round_pairs(pairs[2], 1, 1, 0, [(HALF, round_on_gpsimd)])
-        row3 = round_row(0, 3)
-        round_pairs(pairs[2], 1, 1, HALF, [(C, round_on_gpsimd)])
-        round_pairs(pairs[2], 1, 1, HALF + C, [(C, round_on_gpsimd)])
-        gather_pairs(1, 1, pairs[2], C)
-        gather_row(0, 2, row2)
-        gather_row(0, 3, row3)
-        w_raws = [load_weights(0), load_weights(1), load_weights(2)]
+        round_pairs(pairs[2], 1, 1, HALF, [(HALF, round_on_scalar)], last_raw)
+        weave(0, 2)
+        weave(0, 3)
+        gather_pairs(1, 1, pairs[2])
+        w_raws = [load_weights(e) for e in range(E - 1)]
         gate_sb = keep.tile([P, SLOTS], F32, name="gate_sb")
         nc.sync.dma_start(gate_sb[:], gate)
-        w_raws.append(load_weights(3))
+        w_raws.append(load_weights(E - 1))
         weights = []
 
         own_out = keep.tile([P, T], F32, name="own_out")
@@ -179,17 +201,12 @@ def tile_moe_loc_lin_gelu_kernel(tc, x_words, x_scales, xo, w, gate, offs, offs2
                 )
 
         def multiply(e):
-            cols = slice(e * C, (e + 1) * C)
             weights.append(quantise_weights(e, w_raws[e], round_on_gpsimd if e < 2 else round_on_scalar))
-            x_bf = keep.tile([P, PASSES, C * PACK], BF16, name=f"x_bf{e}", align_bytes=64)
-            nc.scalar.copy(
-                x_bf[:].bitcast(F32).rearrange("p s (c u) -> p s c u", u=2),
-                picked[:].bitcast(F32)[:, :, :, cols].rearrange("p s u c -> p s c u"),
-            )
+            weave(1, e)
             x_codes = keep.tile([P, PASSES * C], U32, name=f"x_codes{e}", align_bytes=64)
             x_planes = keep.tile([P, PASSES * C], U8, name=f"x_planes{e}", align_bytes=64)
             nc.vector.quantize_mx(
-                out=x_codes[:].bitcast(FP8X4), scales=x_planes[:], in_=x_bf[:].rearrange("p s c -> p (s c)")
+                out=x_codes[:].bitcast(FP8X4), scales=x_planes[:], in_=x_bf[e][:].rearrange("p s c -> p (s c)")
             )
             acc = psum.tile([N, C], F32, name=f"own_acc{e}")
             product(
@@ -198,20 +215,18 @@ def tile_moe_loc_lin_gelu_kernel(tc, x_words, x_scales, xo, w, gate, offs, offs2
             )
             return acc
 
-        def finish(e, acc):
-            act = keep.tile([N, C], F32, name=f"act{e}")
-            nc.scalar.activation(act[:], acc[:], GELU)
-            nc.vector.tensor_tensor(
-                own_out[:].indirect(entries(own_list, e * C, C)), act[:], gate_sb[:, e * C : (e + 1) * C], MULT
-            )
-
-        LAG = 1
-        sums = []
-        for step in range(E + LAG):
-            if step < E:
-                sums.append(multiply(step))
-            if step >= LAG:
-                finish(step - LAG, sums[step - LAG])
+        sums = [multiply(e) for e in range(E)]
+        first_act = keep.tile([N, C], F32, name="first_act", tag=f"w_raw{E - 2}")
+        later_act = keep.tile([N, SLOTS], F32, name="later_act", tag=f"w_raw{E - 1}")
+        for e in range(E):
+            cols = slice(e * C, (e + 1) * C)
+            act = first_act[:] if e == 0 else later_act[:, cols]
+            nc.scalar.activation(act, sums[e][:], GELU)
+            if e < 2:
+                nc.vector.tensor_tensor(own_out[:].indirect(entries(own_list, e * C, C)), act, gate_sb[:, cols], MULT)
+        nc.vector.tensor_tensor(
+            own_out[:].indirect(entries(own_list, HALF, HALF)), later_act[:, HALF:], gate_sb[:, HALF:], MULT
+        )
 
         for first in range(0, E, 2):
             far_acc = psum.tile([N, 2, C], F32, name=f"far_acc{first}")
@@ -221,7 +236,9 @@ def tile_moe_loc_lin_gelu_kernel(tc, x_words, x_scales, xo, w, gate, offs, offs2
                     far_acc[:, i, :], first + i,
                     lambda s: far_codes[s][:, cols], lambda s: far_scales[4 * s : P, cols],
                 )
-            far_act = keep.tile([N, 2 * C], F32, name=f"far_act{first}")
+            far_act = keep.tile(
+                [N, 2 * C], F32, name=f"far_act{first}", tag=f"w_bf{E - 1 - first // 2}", align_bytes=64
+            )
             nc.scalar.activation(far_act[:], far_acc[:].rearrange("p i c -> p (i c)"), GELU)
             nc.scalar.dma_start(out[:, T + first * C : T + (first + 2) * C], far_act[:])
         nc.sync.dma_start(out[:, 0:T], own_out[:])

@@ -51,11 +51,12 @@ def tile_moe_loc_lin_gelu_kernel(tc, x_words, x_scales, xo, w, gate, offs, offs2
             nc.sync.dma_start(win[:], x_words[s].rearrange("p t d -> p (t d)").bitcast(I32))
             return win
 
-        def gather_far_words(s, win):
-            codes = keep.tile([P, SLOTS], U32, name=f"far_codes{s}", align_bytes=64)
-            for first in range(0, SLOTS, HALF):
+        def gather_far_words(s, win, slots):
+            codes = keep.tile([P, slots], U32, name=f"far_codes{s}", align_bytes=64)
+            for first in range(0, slots, HALF):
+                count = min(HALF, slots - first)
                 nc.vector.tensor_copy(
-                    codes[:, first : first + HALF], win[:].bitcast(U32).indirect(entries(far_list, first, HALF))
+                    codes[:, first : first + count], win[:].bitcast(U32).indirect(entries(far_list, first, count))
                 )
             return codes
 
@@ -68,16 +69,24 @@ def tile_moe_loc_lin_gelu_kernel(tc, x_words, x_scales, xo, w, gate, offs, offs2
         def pass_rows(s):
             return xo[s * K_PASS : (s + 1) * K_PASS, :].rearrange("(p j) t -> p j t", j=PACK)
 
-        picked = [
-            [keep.tile([P, 2, 2 * HALF], BF16, name=f"picked{s}{h}", align_bytes=64) for h in range(2)]
-            for s in range(PASSES)
-        ]
+        cuts = [[(0, HALF), (HALF, C), (HALF + C, C)], [(0, HALF), (HALF, HALF)]]
+        picked = {}
+
+        def staging(s, first, count):
+            if (s, first) not in picked:
+                tag = "raw10_0" if (s, first) == (0, HALF + C) else f"picked{s}_{first}"
+                picked[s, first] = keep.tile(
+                    [P, 2, 2 * count], BF16, name=f"picked{s}_{first}", tag=tag, align_bytes=64
+                )
+            return picked[s, first]
 
         def round_pairs(pairs, s, u, first, shares, raw=None):
             width = sum(count for count, rounder in shares)
             if raw is None:
-                raw = keep.tile([P, 2, width], F32, name=f"raw{s}{u}_{first}")
-            nc.sync.dma_start(raw[:], pass_rows(s)[:, 2 * u : 2 * u + 2, first : first + width])
+                raw = keep.tile(
+                    [P, 2, width], F32, name=f"raw{s}{u}_{first}", tag=f"raw{s}{u}_{first}", align_bytes=64
+                )[:]
+            nc.sync.dma_start(raw, pass_rows(s)[:, 2 * u : 2 * u + 2, first : first + width])
             done = 0
             for count, rounder in shares:
                 rounder(
@@ -86,11 +95,11 @@ def tile_moe_loc_lin_gelu_kernel(tc, x_words, x_scales, xo, w, gate, offs, offs2
                 )
                 done += count
 
-        def gather_pairs(s, u, pairs):
-            for h in range(2):
+        def gather_pairs(s, u, pairs, pieces):
+            for first, count in pieces:
                 nc.vector.tensor_copy(
-                    picked[s][h][:, u, :].bitcast(U32),
-                    pairs[:].rearrange("p t j -> p (t j)").bitcast(U32).indirect(entries(own_list, h * HALF, HALF)),
+                    staging(s, first, count)[:, u, :].bitcast(U32),
+                    pairs[:].rearrange("p t j -> p (t j)").bitcast(U32).indirect(entries(own_list, first, count)),
                 )
 
         def round_row(s, j, shares):
@@ -103,26 +112,25 @@ def tile_moe_loc_lin_gelu_kernel(tc, x_words, x_scales, xo, w, gate, offs, offs2
                 done += count
             return row
 
-        def gather_row(s, j, row):
-            for h in range(2):
+        def gather_row(s, j, row, pieces):
+            for first, count in pieces:
                 nc.scalar.activation(
-                    picked[s][h][:, j // 2, j % 2 : 2 * HALF : 2],
-                    row[:].indirect(entries(own_list, h * HALF, HALF)),
+                    staging(s, first, count)[:, j // 2, j % 2 : 2 * count : 2],
+                    row[:].indirect(entries(own_list, first, count)),
                     COPY,
                 )
 
-        x_bf = [keep.tile([P, PASSES, C * PACK], BF16, name=f"x_bf{e}", align_bytes=64) for e in range(2)]
-        x_bf += [
-            reuse.tile([P, PASSES, C * PACK], BF16, name=f"x_bf{e}", align_bytes=64, offset=(e - 2) * 4096)
-            for e in range(2, E)
+        x_bf = [
+            reuse.tile([P, PASSES, C * PACK], BF16, name=f"x_bf{e}", align_bytes=64, offset=e * 4096) for e in range(E)
         ]
-        last_raw = reuse.tile([P, 2, HALF], F32, name="last_raw", align_bytes=64, offset=2048)
+        last_raw = reuse.tile([P, 2, 4 * HALF], F32, name="last_raw", align_bytes=64, offset=0)
 
         def weave(s, e):
-            cols = slice(e % 2 * C, (e % 2 + 1) * C)
+            first = max(start for start, count in cuts[s] if start <= e * C)
+            cols = slice(e * C - first, (e + 1) * C - first)
             nc.scalar.copy(
                 x_bf[e][:, s, :].bitcast(F32).rearrange("p (c u) -> p c u", u=2),
-                picked[s][e // 2][:].bitcast(F32)[:, :, cols].rearrange("p u c -> p c u"),
+                picked[s, first][:].bitcast(F32)[:, :, cols].rearrange("p u c -> p c u"),
             )
 
         def load_weights(e):
@@ -155,7 +163,7 @@ def tile_moe_loc_lin_gelu_kernel(tc, x_words, x_scales, xo, w, gate, offs, offs2
                 x_scales[:, 4 * quad : 4 * quad + 4, :].bitcast(I32),
             )
         nc.sync.dma_start(own_list[:], offs)
-        far_codes = [gather_far_words(0, win0)]
+        far_codes = [gather_far_words(0, win0, SLOTS)]
         far_scales = keep.tile([P, SLOTS], U8, name="far_scales", align_bytes=64)
         for first in range(0, SLOTS, HALF):
             nc.vector.tensor_copy(
@@ -163,22 +171,26 @@ def tile_moe_loc_lin_gelu_kernel(tc, x_words, x_scales, xo, w, gate, offs, offs2
             )
 
         pairs = [keep.tile([P, T, 2], BF16, name=f"pairs{i}", align_bytes=64) for i in range(3)]
-        gather_row(0, 2, round_row(0, 2, [(HALF, round_on_scalar), (HALF, round_on_gpsimd)]))
-        gather_row(0, 3, round_row(0, 3, [(T, round_on_gpsimd)]))
+        row2 = round_row(0, 2, [(HALF, round_on_scalar), (HALF, round_on_gpsimd)])
+        gather_row(0, 2, row2, cuts[0][:2])
+        row3 = round_row(0, 3, [(T, round_on_gpsimd)])
+        gather_row(0, 3, row3, cuts[0][:2])
         round_pairs(pairs[0], 0, 0, 0, [(HALF, round_on_gpsimd)])
-        far_codes.append(gather_far_words(1, load_far_words(1)))
+        win1 = load_far_words(1)
+        far_codes.append(gather_far_words(1, win1, SLOTS - C))
         round_pairs(pairs[0], 0, 0, HALF, [(HALF, round_on_gpsimd)])
-        gather_pairs(0, 0, pairs[0])
-        round_pairs(pairs[1], 1, 0, 0, [(HALF, round_on_gpsimd)])
+        gather_pairs(0, 0, pairs[0], cuts[0][:2])
+        round_pairs(pairs[1], 1, 0, 0, [(HALF, round_on_scalar)])
+        gather_pairs(0, 0, pairs[0], cuts[0][2:])
+        gather_row(0, 2, row2, cuts[0][2:])
+        gather_row(0, 3, row3, cuts[0][2:])
         round_pairs(pairs[1], 1, 0, HALF, [(HALF, round_on_gpsimd)])
-        gather_pairs(1, 0, pairs[1])
-        weave(0, 0)
-        weave(0, 1)
+        gather_pairs(1, 0, pairs[1], cuts[1])
         round_pairs(pairs[2], 1, 1, 0, [(HALF, round_on_gpsimd)])
-        round_pairs(pairs[2], 1, 1, HALF, [(HALF, round_on_scalar)], last_raw)
-        weave(0, 2)
-        weave(0, 3)
-        gather_pairs(1, 1, pairs[2])
+        round_pairs(pairs[2], 1, 1, HALF, [(HALF, round_on_scalar)], last_raw[:, :, 0:HALF])
+        for e in range(E):
+            weave(0, e)
+        gather_pairs(1, 1, pairs[2], cuts[1])
         w_raws = [load_weights(e) for e in range(E - 1)]
         gate_sb = keep.tile([P, SLOTS], F32, name="gate_sb")
         nc.sync.dma_start(gate_sb[:], gate)
@@ -200,14 +212,16 @@ def tile_moe_loc_lin_gelu_kernel(tc, x_words, x_scales, xo, w, gate, offs, offs2
                     stop=(s == PASSES - 1),
                 )
 
-        def multiply(e):
-            weights.append(quantise_weights(e, w_raws[e], round_on_gpsimd if e < 2 else round_on_scalar))
+        def quantise_tokens(e):
             weave(1, e)
-            x_codes = keep.tile([P, PASSES * C], U32, name=f"x_codes{e}", align_bytes=64)
+            x_codes = keep.tile([P, PASSES * C], U32, name=f"x_codes{e}", tag=f"x_codes{e}", align_bytes=64)
             x_planes = keep.tile([P, PASSES * C], U8, name=f"x_planes{e}", align_bytes=64)
             nc.vector.quantize_mx(
                 out=x_codes[:].bitcast(FP8X4), scales=x_planes[:], in_=x_bf[e][:].rearrange("p s c -> p (s c)")
             )
+            return x_codes, x_planes
+
+        def multiply(e, x_codes, x_planes):
             acc = psum.tile([N, C], F32, name=f"own_acc{e}")
             product(
                 acc[:], e,
@@ -215,18 +229,28 @@ def tile_moe_loc_lin_gelu_kernel(tc, x_words, x_scales, xo, w, gate, offs, offs2
             )
             return acc
 
-        sums = [multiply(e) for e in range(E)]
-        first_act = keep.tile([N, C], F32, name="first_act", tag=f"w_raw{E - 2}")
-        later_act = keep.tile([N, SLOTS], F32, name="later_act", tag=f"w_raw{E - 1}")
-        for e in range(E):
-            cols = slice(e * C, (e + 1) * C)
-            act = first_act[:] if e == 0 else later_act[:, cols]
-            nc.scalar.activation(act, sums[e][:], GELU)
-            if e < 2:
-                nc.vector.tensor_tensor(own_out[:].indirect(entries(own_list, e * C, C)), act, gate_sb[:, cols], MULT)
-        nc.vector.tensor_tensor(
-            own_out[:].indirect(entries(own_list, HALF, HALF)), later_act[:, HALF:], gate_sb[:, HALF:], MULT
-        )
+        def scatter(first, count, act):
+            nc.vector.tensor_tensor(
+                own_out[:].indirect(entries(own_list, first, count)), act, gate_sb[:, first : first + count], MULT
+            )
+
+        sums = []
+        for e in range(2):
+            weights.append(quantise_weights(e, w_raws[e], round_on_gpsimd))
+            sums.append(multiply(e, *quantise_tokens(e)))
+        tokens = {e: quantise_tokens(e) for e in range(2, E)}
+        for e in range(2, E):
+            weights.append(quantise_weights(e, w_raws[e], round_on_scalar))
+            sums.append(multiply(e, *tokens[e]))
+            act = keep.tile([N, C], F32, name=f"act{e - 2}", tag=f"w_raw{e}")
+            nc.scalar.activation(act[:], sums[e - 2][:], GELU)
+            scatter((e - 2) * C, C, act[:])
+        late_codes = keep.tile([P, C], U32, name="late_codes", tag=f"x_codes{E - 1}", align_bytes=64)
+        nc.vector.tensor_copy(late_codes[:], win1[:].bitcast(U32).indirect(entries(far_list, SLOTS - C, C)))
+        last_act = keep.tile([N, HALF], F32, name="last_act")
+        for e in range(2, E):
+            nc.scalar.activation(last_act[:, (e - 2) * C : (e - 1) * C], sums[e][:], GELU)
+        scatter(HALF, HALF, last_act[:])
 
         for first in range(0, E, 2):
             far_acc = psum.tile([N, 2, C], F32, name=f"far_acc{first}")
@@ -234,7 +258,8 @@ def tile_moe_loc_lin_gelu_kernel(tc, x_words, x_scales, xo, w, gate, offs, offs2
                 cols = slice((first + i) * C, (first + i + 1) * C)
                 product(
                     far_acc[:, i, :], first + i,
-                    lambda s: far_codes[s][:, cols], lambda s: far_scales[4 * s : P, cols],
+                    lambda s: late_codes[:] if (first + i, s) == (E - 1, PASSES - 1) else far_codes[s][:, cols],
+                    lambda s: far_scales[4 * s : P, cols],
                 )
             far_act = keep.tile(
                 [N, 2 * C], F32, name=f"far_act{first}", tag=f"w_bf{E - 1 - first // 2}", align_bytes=64

@@ -120,10 +120,12 @@ def tile_moe_loc_lin_gelu_kernel(tc, x_words, x_scales, xo, w, gate, offs, offs2
                     COPY,
                 )
 
-        x_bf = [
-            reuse.tile([P, PASSES, C * PACK], BF16, name=f"x_bf{e}", align_bytes=64, offset=e * 4096) for e in range(E)
+        x_bf = [keep.tile([P, PASSES, C * PACK], BF16, name=f"x_bf{e}", align_bytes=64) for e in range(2)]
+        x_bf += [
+            reuse.tile([P, PASSES, C * PACK], BF16, name=f"x_bf{e}", align_bytes=64, offset=(e - 2) * 4096)
+            for e in range(2, E)
         ]
-        last_raw = reuse.tile([P, 2, 4 * HALF], F32, name="last_raw", align_bytes=64, offset=0)
+        last_raw = reuse.tile([P, 2, HALF], F32, name="last_raw", align_bytes=64, offset=2048)
 
         def weave(s, e):
             first = max(start for start, count in cuts[s] if start <= e * C)
@@ -177,7 +179,7 @@ def tile_moe_loc_lin_gelu_kernel(tc, x_words, x_scales, xo, w, gate, offs, offs2
         gather_row(0, 3, row3, cuts[0][:2])
         round_pairs(pairs[0], 0, 0, 0, [(HALF, round_on_gpsimd)])
         win1 = load_far_words(1)
-        far_codes.append(gather_far_words(1, win1, SLOTS - C))
+        far_codes.append(gather_far_words(1, win1, SLOTS))
         round_pairs(pairs[0], 0, 0, HALF, [(HALF, round_on_gpsimd)])
         gather_pairs(0, 0, pairs[0], cuts[0][:2])
         round_pairs(pairs[1], 1, 0, 0, [(HALF, round_on_scalar)])
@@ -187,9 +189,11 @@ def tile_moe_loc_lin_gelu_kernel(tc, x_words, x_scales, xo, w, gate, offs, offs2
         round_pairs(pairs[1], 1, 0, HALF, [(HALF, round_on_gpsimd)])
         gather_pairs(1, 0, pairs[1], cuts[1])
         round_pairs(pairs[2], 1, 1, 0, [(HALF, round_on_gpsimd)])
-        round_pairs(pairs[2], 1, 1, HALF, [(HALF, round_on_scalar)], last_raw[:, :, 0:HALF])
-        for e in range(E):
-            weave(0, e)
+        weave(0, 0)
+        weave(0, 1)
+        round_pairs(pairs[2], 1, 1, HALF, [(HALF, round_on_scalar)], last_raw[:])
+        weave(0, 2)
+        weave(0, 3)
         gather_pairs(1, 1, pairs[2], cuts[1])
         w_raws = [load_weights(e) for e in range(E - 1)]
         gate_sb = keep.tile([P, SLOTS], F32, name="gate_sb")
@@ -245,8 +249,6 @@ def tile_moe_loc_lin_gelu_kernel(tc, x_words, x_scales, xo, w, gate, offs, offs2
             act = keep.tile([N, C], F32, name=f"act{e - 2}", tag=f"w_raw{e}")
             nc.scalar.activation(act[:], sums[e - 2][:], GELU)
             scatter((e - 2) * C, C, act[:])
-        late_codes = keep.tile([P, C], U32, name="late_codes", tag=f"x_codes{E - 1}", align_bytes=64)
-        nc.vector.tensor_copy(late_codes[:], win1[:].bitcast(U32).indirect(entries(far_list, SLOTS - C, C)))
         last_act = keep.tile([N, HALF], F32, name="last_act")
         for e in range(2, E):
             nc.scalar.activation(last_act[:, (e - 2) * C : (e - 1) * C], sums[e][:], GELU)
@@ -258,8 +260,7 @@ def tile_moe_loc_lin_gelu_kernel(tc, x_words, x_scales, xo, w, gate, offs, offs2
                 cols = slice((first + i) * C, (first + i + 1) * C)
                 product(
                     far_acc[:, i, :], first + i,
-                    lambda s: late_codes[:] if (first + i, s) == (E - 1, PASSES - 1) else far_codes[s][:, cols],
-                    lambda s: far_scales[4 * s : P, cols],
+                    lambda s: far_codes[s][:, cols], lambda s: far_scales[4 * s : P, cols],
                 )
             far_act = keep.tile(
                 [N, 2 * C], F32, name=f"far_act{first}", tag=f"w_bf{E - 1 - first // 2}", align_bytes=64

@@ -173,7 +173,7 @@ def tile_moe_loc_lin_gelu_kernel(tc, x_words, x_scales, xo, w, gate, offs, offs2
             )
 
         pairs = [keep.tile([P, T, 2], BF16, name=f"pairs{i}", align_bytes=64) for i in range(3)]
-        row2 = round_row(0, 2, [(HALF, round_on_scalar), (HALF, round_on_gpsimd)])
+        row2 = round_row(0, 2, [(640, round_on_scalar), (384, round_on_gpsimd)])
         gather_row(0, 2, row2, cuts[0][:2])
         row3 = round_row(0, 3, [(T, round_on_gpsimd)])
         gather_row(0, 3, row3, cuts[0][:2])
@@ -191,7 +191,7 @@ def tile_moe_loc_lin_gelu_kernel(tc, x_words, x_scales, xo, w, gate, offs, offs2
         round_pairs(pairs[2], 1, 1, 0, [(HALF, round_on_gpsimd)])
         weave(0, 0)
         weave(0, 1)
-        round_pairs(pairs[2], 1, 1, HALF, [(HALF, round_on_scalar)], last_raw[:])
+        round_pairs(pairs[2], 1, 1, HALF, [(384, round_on_scalar), (128, round_on_gpsimd)], last_raw[:])
         weave(0, 2)
         weave(0, 3)
         gather_pairs(1, 1, pairs[2], cuts[1])

@@ -23,6 +23,10 @@ K_PASS = P * PACK
 PASSES = K // K_PASS
 SLOTS = E * C
 HALF = 512
+ALIGN = 256
+ROW_SHARE = 640
+PAIR_SHARE = 352
+OVERLAP = 16
 
 
 def tile_moe_loc_lin_gelu_kernel(tc, x_words, x_scales, xo, w, gate, offs, offs2, out):
@@ -31,6 +35,9 @@ def tile_moe_loc_lin_gelu_kernel(tc, x_words, x_scales, xo, w, gate, offs, offs2
         keep = ctx.enter_context(tc.tile_pool(name="keep", bufs=1))
         reuse = ctx.enter_context(tc.tile_pool(name="reuse", bufs=1))
         psum = ctx.enter_context(tc.psum_pool(name="psum", bufs=1))
+
+        def tile(shape, dtype, name, tag=None):
+            return keep.tile(shape, dtype, name=name, tag=tag or name, align_bytes=ALIGN)
 
         def entries(lst, first, count):
             return lst[:, first // 16 : (first + count) // 16]
@@ -43,22 +50,21 @@ def tile_moe_loc_lin_gelu_kernel(tc, x_words, x_scales, xo, w, gate, offs, offs2
         nc.vector.memset(warm_in[:], 0.0)
         nc.scalar.activation(warm_out[:], warm_in[:], GELU)
 
-        far_scale_win = keep.tile([P, Q], U8, name="far_scale_win", align_bytes=64)
-        nc.vector.memset(far_scale_win[:].bitcast(I32), 0)
+        far_scale_win = tile([P, Q], U8, "far_scale_win")
+        nc.gpsimd.memset(far_scale_win[32:64, :].bitcast(I32), 0)
+        nc.gpsimd.memset(far_scale_win[64:P, :].bitcast(I32), 0)
+        far_scales = tile([P, SLOTS], U8, "far_scales")
+        nc.gpsimd.memset(far_scales[:].bitcast(I32), 0)
 
-        def load_far_words(s):
-            win = keep.tile([P, Q], I32, name=f"far_word_win{s}", align_bytes=64)
+        def gather_far(dst, window):
+            for first in range(0, SLOTS, HALF):
+                nc.vector.tensor_copy(dst[:, first : first + HALF], window.indirect(entries(far_list, first, HALF)))
+
+        def far_words(s):
+            win = tile([P, Q], I32, f"far_word_win{s}")
             nc.sync.dma_start(win[:], x_words[s].rearrange("p t d -> p (t d)").bitcast(I32))
-            return win
-
-        def gather_far_words(s, win, slots):
-            codes = keep.tile([P, slots], U32, name=f"far_codes{s}", align_bytes=64)
-            for first in range(0, slots, HALF):
-                count = min(HALF, slots - first)
-                nc.vector.tensor_copy(
-                    codes[:, first : first + count], win[:].bitcast(U32).indirect(entries(far_list, first, count))
-                )
-            return codes
+            codes = tile([P, SLOTS], U32, f"far_codes{s}")
+            return win, codes
 
         def round_on_scalar(dst, src):
             nc.scalar.copy(dst, src)
@@ -69,139 +75,130 @@ def tile_moe_loc_lin_gelu_kernel(tc, x_words, x_scales, xo, w, gate, offs, offs2
         def pass_rows(s):
             return xo[s * K_PASS : (s + 1) * K_PASS, :].rearrange("(p j) t -> p j t", j=PACK)
 
-        cuts = [[(0, HALF), (HALF, C), (HALF + C, C)], [(0, HALF), (HALF, HALF)]]
-        picked = {}
+        picked = [[tile([P, 2, 2 * HALF], BF16, f"picked{s}{h}") for h in range(2)] for s in range(PASSES)]
 
-        def staging(s, first, count):
-            if (s, first) not in picked:
-                tag = "raw10_0" if (s, first) == (0, HALF + C) else f"picked{s}_{first}"
-                picked[s, first] = keep.tile(
-                    [P, 2, 2 * count], BF16, name=f"picked{s}_{first}", tag=tag, align_bytes=64
-                )
-            return picked[s, first]
-
-        def round_pairs(pairs, s, u, first, shares, raw=None):
-            width = sum(count for count, rounder in shares)
-            if raw is None:
-                raw = keep.tile(
-                    [P, 2, width], F32, name=f"raw{s}{u}_{first}", tag=f"raw{s}{u}_{first}", align_bytes=64
-                )[:]
-            nc.sync.dma_start(raw, pass_rows(s)[:, 2 * u : 2 * u + 2, first : first + width])
+        def round_pairs(pairs, s, u, first, shares, raw):
+            nc.sync.dma_start(raw, pass_rows(s)[:, 2 * u : 2 * u + 2, first : first + HALF])
             done = 0
             for count, rounder in shares:
                 rounder(
-                    pairs[:, first + done : first + done + count, :],
+                    pairs[:, 2 * (first + done) : 2 * (first + done + count)].rearrange("p (t j) -> p t j", j=2),
                     raw[:, :, done : done + count].rearrange("p j t -> p t j"),
                 )
                 done += count
 
-        def gather_pairs(s, u, pairs, pieces):
-            for first, count in pieces:
+        def raw_pairs(name):
+            return tile([P, 2, HALF], F32, name)[:]
+
+        def gather_pairs(s, u, pairs):
+            for h in range(2):
                 nc.vector.tensor_copy(
-                    staging(s, first, count)[:, u, :].bitcast(U32),
-                    pairs[:].rearrange("p t j -> p (t j)").bitcast(U32).indirect(entries(own_list, first, count)),
+                    picked[s][h][:, u, :].bitcast(U32), pairs.bitcast(U32).indirect(entries(own_list, h * HALF, HALF))
                 )
 
-        def round_row(s, j, shares):
-            raw = keep.tile([P, T], F32, name=f"raw_row{s}{j}")
-            nc.sync.dma_start(raw[:], pass_rows(s)[:, j, :])
-            row = keep.tile([P, T], BF16, name=f"row{s}{j}", align_bytes=64)
+        def round_row(row, j, shares):
+            raw = tile([P, T], F32, f"raw_row{j}")
+            nc.sync.dma_start(raw[:], pass_rows(0)[:, j, :])
             done = 0
             for count, rounder in shares:
                 rounder(row[:, done : done + count], raw[:, done : done + count])
                 done += count
-            return row
 
-        def gather_row(s, j, row, pieces):
-            for first, count in pieces:
-                nc.scalar.activation(
-                    staging(s, first, count)[:, j // 2, j % 2 : 2 * count : 2],
-                    row[:].indirect(entries(own_list, first, count)),
-                    COPY,
-                )
+        def gather_row(j, h, window):
+            nc.scalar.activation(
+                picked[0][h][:, 1, j % 2 : 2 * HALF : 2], window.indirect(entries(own_list, h * HALF, HALF)), COPY
+            )
 
-        x_bf = [keep.tile([P, PASSES, C * PACK], BF16, name=f"x_bf{e}", align_bytes=64) for e in range(2)]
-        x_bf += [
-            reuse.tile([P, PASSES, C * PACK], BF16, name=f"x_bf{e}", align_bytes=64, offset=(e - 2) * 4096)
-            for e in range(2, E)
-        ]
-        last_raw = reuse.tile([P, 2, HALF], F32, name="last_raw", align_bytes=64, offset=2048)
+        woven = PASSES * C * PACK
+        x_early = reuse.tile([P, 3 * woven], BF16, name="x_early", align_bytes=ALIGN, offset=0)
+        x_bf = {e: x_early[:, e * woven : (e + 1) * woven] for e in range(3)}
+        last_raw = reuse.tile([P, 2, HALF], F32, name="last_raw", align_bytes=ALIGN, offset=0)
 
         def weave(s, e):
-            first = max(start for start, count in cuts[s] if start <= e * C)
-            cols = slice(e * C - first, (e + 1) * C - first)
+            cols = slice(e % 2 * C, (e % 2 + 1) * C)
             nc.scalar.copy(
-                x_bf[e][:, s, :].bitcast(F32).rearrange("p (c u) -> p c u", u=2),
-                picked[s, first][:].bitcast(F32)[:, :, cols].rearrange("p u c -> p c u"),
+                x_bf[e][:, s * C * PACK : (s + 1) * C * PACK].bitcast(F32).rearrange("p (c u) -> p c u", u=2),
+                picked[s][e // 2][:].bitcast(F32)[:, :, cols].rearrange("p u c -> p c u"),
             )
 
         def load_weights(e):
-            w_raw = keep.tile([P, PASSES, PACK, N], F32, name=f"w_raw{e}", tag=f"w_raw{e}")
+            if e == 2:
+                w_raw = reuse.tile([P, PASSES, PACK, N], F32, name="w_raw2", align_bytes=ALIGN, offset=12288)
+            else:
+                w_raw = tile([P, PASSES, PACK, N], F32, f"w_raw{e}")
             nc.sync.dma_start(w_raw[:], w[e].rearrange("(s p j) n -> p s j n", s=PASSES, j=PACK))
             return w_raw
 
-        def quantise_weights(e, w_raw, rounder):
-            w_bf = keep.tile([P, PASSES, N, PACK], BF16, name=f"w_bf{e}", tag=f"w_bf{e}", align_bytes=64)
-            if rounder is round_on_gpsimd:
-                rounder(w_bf[:], w_raw[:].rearrange("p s j n -> p s n j"))
-            else:
-                for s in range(PASSES):
-                    rounder(
-                        w_bf[:, s, :, :].rearrange("p (c i) j -> p c j i", i=4),
-                        w_raw[:, s, :, :].rearrange("p j (c i) -> p c j i", i=4),
-                    )
-            w_codes = keep.tile([P, PASSES * N], U32, name=f"w_codes{e}", align_bytes=64)
-            w_scales = keep.tile([P, PASSES * N], U8, name=f"w_scales{e}", align_bytes=64)
+        def load_gate(h):
+            part = tile([P, HALF], F32, f"gate{h}")
+            nc.sync.dma_start(part[:], gate[:, h * HALF : (h + 1) * HALF])
+            return part
+
+        weights = {}
+
+        def quantise_weights(e, passes_on_gpsimd):
+            w_raw = w_raws[e]
+            w_bf = tile([P, PASSES, N, PACK], BF16, f"w_bf{e}")
+            if passes_on_gpsimd:
+                round_on_gpsimd(
+                    w_bf[:, 0:passes_on_gpsimd, :, :], w_raw[:, 0:passes_on_gpsimd, :, :].rearrange("p s j n -> p s n j")
+                )
+            for s in range(passes_on_gpsimd, PASSES):
+                round_on_scalar(
+                    w_bf[:, s, :, :].rearrange("p (c i) j -> p c j i", i=4),
+                    w_raw[:, s, :, :].rearrange("p j (c i) -> p c j i", i=4),
+                )
+            w_codes = tile([P, PASSES * N], U32, f"w_codes{e}")
+            w_scales = tile([P, PASSES * N], U8, f"w_scales{e}")
             nc.vector.quantize_mx(
                 out=w_codes[:].bitcast(FP8X4), scales=w_scales[:], in_=w_bf[:].rearrange("p s n j -> p (s n j)")
             )
-            return w_codes, w_scales
+            weights[e] = (w_codes, w_scales)
+
+        planes = tile([P, T + 2 * 2 * T], BF16, "planes")
+        row3, pair_a, pair_b = planes[:, 0:T], planes[:, T : 3 * T], planes[:, 3 * T : 5 * T]
+        row2 = tile([P, T], BF16, "row2")[:]
+        pair_c = tile([P, 2 * T], BF16, "pair_c")[:]
+        whole = [(HALF, round_on_gpsimd)]
+        shared = [(HALF - PAIR_SHARE, round_on_gpsimd), (PAIR_SHARE, round_on_scalar)]
 
         nc.sync.dma_start(far_list[:], offs2)
-        win0 = load_far_words(0)
-        for quad in range(4):
-            nc.sync.dma_start(
-                far_scale_win[32 * quad : 32 * quad + 4 * PASSES, :].bitcast(I32),
-                x_scales[:, 4 * quad : 4 * quad + 4, :].bitcast(I32),
-            )
+        nc.sync.dma_start(far_scale_win[0:32, :].bitcast(I32), x_scales.rearrange("s b t -> (s b) t").bitcast(I32))
+        win0, codes0 = far_words(0)
         nc.sync.dma_start(own_list[:], offs)
-        far_codes = [gather_far_words(0, win0, SLOTS)]
-        far_scales = keep.tile([P, SLOTS], U8, name="far_scales", align_bytes=64)
-        for first in range(0, SLOTS, HALF):
-            nc.vector.tensor_copy(
-                far_scales[:, first : first + HALF], far_scale_win[:].indirect(entries(far_list, first, HALF))
-            )
+        scale_rows = tile([P, SLOTS], U8, "scale_rows")
+        gather_far(scale_rows, far_scale_win[:])
+        gather_far(codes0, win0[:].bitcast(U32))
 
-        pairs = [keep.tile([P, T, 2], BF16, name=f"pairs{i}", align_bytes=64) for i in range(3)]
-        row2 = round_row(0, 2, [(640, round_on_scalar), (384, round_on_gpsimd)])
-        gather_row(0, 2, row2, cuts[0][:2])
-        row3 = round_row(0, 3, [(T, round_on_gpsimd)])
-        gather_row(0, 3, row3, cuts[0][:2])
-        round_pairs(pairs[0], 0, 0, 0, [(HALF, round_on_gpsimd)])
-        win1 = load_far_words(1)
-        far_codes.append(gather_far_words(1, win1, SLOTS))
-        round_pairs(pairs[0], 0, 0, HALF, [(HALF, round_on_gpsimd)])
-        gather_pairs(0, 0, pairs[0], cuts[0][:2])
-        round_pairs(pairs[1], 1, 0, 0, [(HALF, round_on_scalar)])
-        gather_pairs(0, 0, pairs[0], cuts[0][2:])
-        gather_row(0, 2, row2, cuts[0][2:])
-        gather_row(0, 3, row3, cuts[0][2:])
-        round_pairs(pairs[1], 1, 0, HALF, [(HALF, round_on_gpsimd)])
-        gather_pairs(1, 0, pairs[1], cuts[1])
-        round_pairs(pairs[2], 1, 1, 0, [(HALF, round_on_gpsimd)])
-        weave(0, 0)
-        weave(0, 1)
-        round_pairs(pairs[2], 1, 1, HALF, [(384, round_on_scalar), (128, round_on_gpsimd)], last_raw[:])
-        weave(0, 2)
-        weave(0, 3)
-        gather_pairs(1, 1, pairs[2], cuts[1])
-        w_raws = [load_weights(e) for e in range(E - 1)]
-        gate_sb = keep.tile([P, SLOTS], F32, name="gate_sb")
-        nc.sync.dma_start(gate_sb[:], gate)
-        w_raws.append(load_weights(E - 1))
-        weights = []
+        round_row(row2, 2, [(ROW_SHARE, round_on_scalar), (T - ROW_SHARE, round_on_gpsimd)])
+        gather_row(2, 0, row2)
+        gather_row(2, 1, row2)
+        round_pairs(pair_a, 0, 0, HALF, whole, raw_pairs("raw_a1"))
+        win1, codes1 = far_words(1)
+        gather_far(codes1, win1[:].bitcast(U32))
+        far_codes = [codes0, codes1]
+        round_row(row3, 3, [(T, round_on_gpsimd)])
+        round_pairs(pair_a, 0, 0, 0, shared, raw_pairs("raw_a0"))
+        gather_pairs(0, 0, pair_a)
+        gather_row(3, 0, planes[:, 0 : T + OVERLAP])
+        round_pairs(pair_b, 1, 0, HALF, whole, raw_pairs("raw_b1"))
+        round_pairs(pair_b, 1, 0, 0, shared, raw_pairs("raw_b0"))
+        gather_pairs(1, 0, pair_b)
+        gather_row(3, 1, planes[:, 0 : 3 * T + OVERLAP])
+        round_pairs(pair_c, 1, 1, HALF, whole, raw_pairs("raw_c1"))
+        round_pairs(pair_c, 1, 1, 0, shared, last_raw[:])
+        gather_pairs(1, 1, pair_c)
 
-        own_out = keep.tile([P, T], F32, name="own_out")
+        w_raws = [load_weights(e) for e in range(2)]
+        gates = [load_gate(0)]
+        w_raws += [load_weights(e) for e in range(2, E)]
+        for s in range(PASSES):
+            for quad in range(4):
+                to, src = 32 * quad + 4 * s, 16 * s + 4 * quad
+                nc.sync.dma_start(far_scales[to : to + 4, :].bitcast(I32), scale_rows[src : src + 4, :].bitcast(I32))
+        gates.append(load_gate(1))
+
+        own_out = tile([P, T], F32, "own_out")
 
         def product(acc, e, codes, scales):
             w_codes, w_scales = weights[e]
@@ -216,55 +213,80 @@ def tile_moe_loc_lin_gelu_kernel(tc, x_words, x_scales, xo, w, gate, offs, offs2
                     stop=(s == PASSES - 1),
                 )
 
-        def quantise_tokens(e):
-            weave(1, e)
-            x_codes = keep.tile([P, PASSES * C], U32, name=f"x_codes{e}", tag=f"x_codes{e}", align_bytes=64)
-            x_planes = keep.tile([P, PASSES * C], U8, name=f"x_planes{e}", align_bytes=64)
-            nc.vector.quantize_mx(
-                out=x_codes[:].bitcast(FP8X4), scales=x_planes[:], in_=x_bf[e][:].rearrange("p s c -> p (s c)")
-            )
-            return x_codes, x_planes
+        tokens = {}
 
-        def multiply(e, x_codes, x_planes):
-            acc = psum.tile([N, C], F32, name=f"own_acc{e}")
+        def quantise_tokens(e):
+            x_codes = tile([P, PASSES * C], U32, f"x_codes{e}")
+            x_planes = tile([P, PASSES * C], U8, f"x_planes{e}")
+            nc.vector.quantize_mx(
+                out=x_codes[:].bitcast(FP8X4), scales=x_planes[:], in_=x_bf[e]
+            )
+            tokens[e] = (x_codes, x_planes)
+
+        sums = {}
+        banks = [psum.tile([N, 2, C], F32, name=f"bank{b}") for b in range(E + 1)]
+        far_sums = [banks[2][:, 1, :], banks[3][:, 1, :], banks[E][:, 0, :], banks[E][:, 1, :]]
+
+        def multiply_far(e):
+            cols = slice(e * C, (e + 1) * C)
+            product(far_sums[e], e, lambda s: far_codes[s][:, cols], lambda s: far_scales[4 * s : P, cols])
+
+        def multiply(e):
+            x_codes, x_planes = tokens[e]
+            sums[e] = banks[e][:, 0, :]
             product(
-                acc[:], e,
+                sums[e], e,
                 lambda s: x_codes[:, s * C : (s + 1) * C], lambda s: x_planes[:, s * C : (s + 1) * C],
             )
-            return acc
 
-        def scatter(first, count, act):
+        def give_back(e):
+            if e == 1:
+                act = reuse.tile([N, C], F32, name="act1", align_bytes=ALIGN, offset=12288)
+            else:
+                act = tile([N, C], F32, f"act{e}")
+            nc.scalar.activation(act[:], sums[e], GELU)
             nc.vector.tensor_tensor(
-                own_out[:].indirect(entries(own_list, first, count)), act, gate_sb[:, first : first + count], MULT
+                own_out[:].indirect(entries(own_list, e * C, C)),
+                act[:],
+                gates[e // 2][:, e % 2 * C : (e % 2 + 1) * C],
+                MULT,
             )
 
-        sums = []
+        for e in range(3):
+            weave(0, e)
         for e in range(2):
-            weights.append(quantise_weights(e, w_raws[e], round_on_gpsimd))
-            sums.append(multiply(e, *quantise_tokens(e)))
-        tokens = {e: quantise_tokens(e) for e in range(2, E)}
-        for e in range(2, E):
-            weights.append(quantise_weights(e, w_raws[e], round_on_scalar))
-            sums.append(multiply(e, *tokens[e]))
-            act = keep.tile([N, C], F32, name=f"act{e - 2}", tag=f"w_raw{e}")
-            nc.scalar.activation(act[:], sums[e - 2][:], GELU)
-            scatter((e - 2) * C, C, act[:])
-        last_act = keep.tile([N, HALF], F32, name="last_act")
-        for e in range(2, E):
-            nc.scalar.activation(last_act[:, (e - 2) * C : (e - 1) * C], sums[e][:], GELU)
-        scatter(HALF, HALF, last_act[:])
+            weave(1, e)
+        quantise_weights(0, 2)
+        quantise_tokens(0)
+        multiply(0)
+        quantise_tokens(1)
+        quantise_weights(1, 1)
+        multiply(1)
+        weave(1, 2)
+        quantise_tokens(2)
+        give_back(0)
+        quantise_weights(2, 0)
+        multiply_far(0)
+        multiply(2)
+        give_back(1)
+        x_last = reuse.tile([P, woven], BF16, name="x_last", align_bytes=ALIGN, offset=12288 + 1024)
+        x_bf[3] = x_last[:]
+        for s in range(PASSES):
+            weave(s, 3)
+        quantise_tokens(3)
+        quantise_weights(3, 0)
+        multiply_far(1)
+        multiply(3)
+        give_back(2)
+        give_back(3)
+        multiply_far(2)
+        multiply_far(3)
 
-        for first in range(0, E, 2):
-            far_acc = psum.tile([N, 2, C], F32, name=f"far_acc{first}")
-            for i in range(2):
-                cols = slice((first + i) * C, (first + i + 1) * C)
-                product(
-                    far_acc[:, i, :], first + i,
-                    lambda s: far_codes[s][:, cols], lambda s: far_scales[4 * s : P, cols],
-                )
-            far_act = keep.tile(
-                [N, 2 * C], F32, name=f"far_act{first}", tag=f"w_bf{E - 1 - first // 2}", align_bytes=64
-            )
-            nc.scalar.activation(far_act[:], far_acc[:].rearrange("p i c -> p (i c)"), GELU)
-            nc.scalar.dma_start(out[:, T + first * C : T + (first + 2) * C], far_act[:])
+        first_act = tile([N, 2, C], F32, "far_act0", tag="w_bf3")
+        for e in range(2):
+            nc.scalar.activation(first_act[:, e, :], far_sums[e], GELU)
+        nc.scalar.dma_start(out[:, T : T + HALF], first_act[:].rearrange("p i c -> p (i c)"))
+        second_act = tile([N, HALF], F32, "far_act1")
+        nc.scalar.activation(second_act[:], banks[E][:].rearrange("p i c -> p (i c)"), GELU)
+        nc.scalar.dma_start(out[:, T + HALF : T + SLOTS], second_act[:])
         nc.sync.dma_start(out[:, 0:T], own_out[:])

@@ -47,14 +47,14 @@ def tile_moe_loc_lin_gelu_kernel(tc, x_words, x_scales, xo, w, gate, offs, offs2
 
         warm_in = keep.tile([P, 8], F32, name="warm_in")
         warm_out = keep.tile([P, 8], F32, name="warm_out")
-        nc.vector.memset(warm_in[:], 0.0)
-        nc.scalar.activation(warm_out[:], warm_in[:], GELU)
 
         far_scale_win = tile([P, Q], U8, "far_scale_win")
         nc.gpsimd.memset(far_scale_win[32:64, :].bitcast(I32), 0)
         nc.gpsimd.memset(far_scale_win[64:P, :].bitcast(I32), 0)
         far_scales = tile([P, SLOTS], U8, "far_scales")
         nc.gpsimd.memset(far_scales[:].bitcast(I32), 0)
+        nc.gpsimd.memset(warm_in[:], 0.0)
+        nc.scalar.activation(warm_out[:], warm_in[:], GELU)
 
         def gather_far(dst, window):
             for first in range(0, SLOTS, HALF):
@@ -96,9 +96,9 @@ def tile_moe_loc_lin_gelu_kernel(tc, x_words, x_scales, xo, w, gate, offs, offs2
                     picked[s][h][:, u, :].bitcast(U32), pairs.bitcast(U32).indirect(entries(own_list, h * HALF, HALF))
                 )
 
-        def round_row(row, j, shares):
+        def round_row(row, j, shares, queue):
             raw = tile([P, T], F32, f"raw_row{j}")
-            nc.sync.dma_start(raw[:], pass_rows(0)[:, j, :])
+            queue.dma_start(raw[:], pass_rows(0)[:, j, :])
             done = 0
             for count, rounder in shares:
                 rounder(row[:, done : done + count], raw[:, done : done + count])
@@ -164,20 +164,20 @@ def tile_moe_loc_lin_gelu_kernel(tc, x_words, x_scales, xo, w, gate, offs, offs2
 
         nc.sync.dma_start(far_list[:], offs2)
         nc.sync.dma_start(far_scale_win[0:32, :].bitcast(I32), x_scales.rearrange("s b t -> (s b) t").bitcast(I32))
-        win0, codes0 = far_words(0)
+        round_row(row2, 2, [(ROW_SHARE, round_on_scalar), (T - ROW_SHARE, round_on_gpsimd)], nc.sync)
         nc.sync.dma_start(own_list[:], offs)
+        win0, codes0 = far_words(0)
         scale_rows = tile([P, SLOTS], U8, "scale_rows")
         gather_far(scale_rows, far_scale_win[:])
         gather_far(codes0, win0[:].bitcast(U32))
 
-        round_row(row2, 2, [(ROW_SHARE, round_on_scalar), (T - ROW_SHARE, round_on_gpsimd)])
         gather_row(2, 0, row2)
         gather_row(2, 1, row2)
         round_pairs(pair_a, 0, 0, HALF, whole, raw_pairs("raw_a1"))
         win1, codes1 = far_words(1)
         gather_far(codes1, win1[:].bitcast(U32))
         far_codes = [codes0, codes1]
-        round_row(row3, 3, [(T, round_on_gpsimd)])
+        round_row(row3, 3, [(T, round_on_gpsimd)], nc.sync)
         round_pairs(pair_a, 0, 0, 0, shared, raw_pairs("raw_a0"))
         gather_pairs(0, 0, pair_a)
         gather_row(3, 0, planes[:, 0 : T + OVERLAP])
@@ -190,12 +190,19 @@ def tile_moe_loc_lin_gelu_kernel(tc, x_words, x_scales, xo, w, gate, offs, offs2
         gather_pairs(1, 1, pair_c)
 
         w_raws = [load_weights(e) for e in range(2)]
-        gates = [load_gate(0)]
-        w_raws += [load_weights(e) for e in range(2, E)]
-        for s in range(PASSES):
-            for quad in range(4):
-                to, src = 32 * quad + 4 * s, 16 * s + 4 * quad
+
+        def place_scale_rows(blocks):
+            for block in blocks:
+                s, quad = divmod(block, 4)
+                to, src = 32 * quad + 4 * s, 4 * block
                 nc.sync.dma_start(far_scales[to : to + 4, :].bitcast(I32), scale_rows[src : src + 4, :].bitcast(I32))
+
+        place_scale_rows(range(0, 3))
+        gates = [load_gate(0)]
+        place_scale_rows(range(3, 6))
+        w_raws.append(load_weights(2))
+        place_scale_rows(range(6, 8))
+        w_raws.append(load_weights(3))
         gates.append(load_gate(1))
 
         own_out = tile([P, T], F32, "own_out")
@@ -243,7 +250,7 @@ def tile_moe_loc_lin_gelu_kernel(tc, x_words, x_scales, xo, w, gate, offs, offs2
             if e == 1:
                 act = reuse.tile([N, C], F32, name="act1", align_bytes=ALIGN, offset=12288)
             else:
-                act = tile([N, C], F32, f"act{e}")
+                act = tile([N, C], F32, f"act{e}", tag="w_raw3" if e == 2 else None)
             nc.scalar.activation(act[:], sums[e], GELU)
             nc.vector.tensor_tensor(
                 own_out[:].indirect(entries(own_list, e * C, C)),
@@ -282,7 +289,7 @@ def tile_moe_loc_lin_gelu_kernel(tc, x_words, x_scales, xo, w, gate, offs, offs2
         multiply_far(2)
         multiply_far(3)
 
-        first_act = tile([N, 2, C], F32, "far_act0", tag="w_bf3")
+        first_act = tile([N, 2, C], F32, "far_act0", tag="x_codes3")
         for e in range(2):
             nc.scalar.activation(first_act[:, e, :], far_sums[e], GELU)
         nc.scalar.dma_start(out[:, T : T + HALF], first_act[:].rearrange("p i c -> p (i c)"))

@@ -49,11 +49,11 @@ def tile_moe_loc_lin_gelu_kernel(tc, x_words, x_scales, xo, w, gate, offs, offs2
         warm_out = keep.tile([P, 8], F32, name="warm_out")
 
         far_scale_win = tile([P, Q], U8, "far_scale_win")
-        nc.gpsimd.memset(far_scale_win[32:64, :].bitcast(I32), 0)
-        nc.gpsimd.memset(far_scale_win[64:P, :].bitcast(I32), 0)
+        nc.vector.memset(warm_in[:], 0.0)
+        nc.vector.memset(far_scale_win[32:64, :].bitcast(I32), 0)
+        nc.vector.memset(far_scale_win[64:P, :].bitcast(I32), 0)
         far_scales = tile([P, SLOTS], U8, "far_scales")
-        nc.gpsimd.memset(far_scales[:].bitcast(I32), 0)
-        nc.gpsimd.memset(warm_in[:], 0.0)
+        nc.vector.memset(far_scales[:].bitcast(I32), 0)
         nc.scalar.activation(warm_out[:], warm_in[:], GELU)
 
         def gather_far(dst, window):

@@ -25,8 +25,9 @@ SLOTS = E * C
 HALF = 512
 ALIGN = 256
 ROW_SHARE = 640
-PAIR_SHARE = 352
+PAIR_SHARE = 320
 OVERLAP = 16
+LATE = 128
 
 
 def tile_moe_loc_lin_gelu_kernel(tc, x_words, x_scales, xo, w, gate, offs, offs2, out):
@@ -56,9 +57,10 @@ def tile_moe_loc_lin_gelu_kernel(tc, x_words, x_scales, xo, w, gate, offs, offs2
         nc.vector.memset(far_scales[:].bitcast(I32), 0)
         nc.scalar.activation(warm_out[:], warm_in[:], GELU)
 
-        def gather_far(dst, window):
-            for first in range(0, SLOTS, HALF):
-                nc.vector.tensor_copy(dst[:, first : first + HALF], window.indirect(entries(far_list, first, HALF)))
+        def gather_far(dst, window, slots=SLOTS):
+            for first in range(0, slots, HALF):
+                count = min(HALF, slots - first)
+                nc.vector.tensor_copy(dst[:, first : first + count], window.indirect(entries(far_list, first, count)))
 
         def far_words(s):
             win = tile([P, Q], I32, f"far_word_win{s}")
@@ -75,7 +77,13 @@ def tile_moe_loc_lin_gelu_kernel(tc, x_words, x_scales, xo, w, gate, offs, offs2
         def pass_rows(s):
             return xo[s * K_PASS : (s + 1) * K_PASS, :].rearrange("(p j) t -> p j t", j=PACK)
 
-        picked = [[tile([P, 2, 2 * HALF], BF16, f"picked{s}{h}") for h in range(2)] for s in range(PASSES)]
+        picked_early = tile([P, 4 * SLOTS], BF16, "picked0")
+        picked_late = [tile([P, 4 * HALF], BF16, f"picked1{h}") for h in range(2)]
+
+        def staged(s, first):
+            if s == 0:
+                return picked_early[:], first, SLOTS
+            return picked_late[first // HALF][:], first % HALF, HALF
 
         def round_pairs(pairs, s, u, first, shares, raw):
             nc.sync.dma_start(raw, pass_rows(s)[:, 2 * u : 2 * u + 2, first : first + HALF])
@@ -91,9 +99,11 @@ def tile_moe_loc_lin_gelu_kernel(tc, x_words, x_scales, xo, w, gate, offs, offs2
             return tile([P, 2, HALF], F32, name)[:]
 
         def gather_pairs(s, u, pairs):
-            for h in range(2):
+            for first in range(0, SLOTS, HALF):
+                dst, at, width = staged(s, first)
                 nc.vector.tensor_copy(
-                    picked[s][h][:, u, :].bitcast(U32), pairs.bitcast(U32).indirect(entries(own_list, h * HALF, HALF))
+                    dst.bitcast(U32)[:, u * width + at : u * width + at + HALF],
+                    pairs.bitcast(U32).indirect(entries(own_list, first, HALF)),
                 )
 
         def round_row(row, j, shares, queue):
@@ -104,9 +114,12 @@ def tile_moe_loc_lin_gelu_kernel(tc, x_words, x_scales, xo, w, gate, offs, offs2
                 rounder(row[:, done : done + count], raw[:, done : done + count])
                 done += count
 
-        def gather_row(j, h, window):
+        def gather_row(j, first, count, window):
+            start = 2 * (SLOTS + first)
             nc.scalar.activation(
-                picked[0][h][:, 1, j % 2 : 2 * HALF : 2], window.indirect(entries(own_list, h * HALF, HALF)), COPY
+                picked_early[:, start + j % 2 : start + 2 * count : 2],
+                window.indirect(entries(own_list, first, count)),
+                COPY,
             )
 
         woven = PASSES * C * PACK
@@ -115,10 +128,10 @@ def tile_moe_loc_lin_gelu_kernel(tc, x_words, x_scales, xo, w, gate, offs, offs2
         last_raw = reuse.tile([P, 2, HALF], F32, name="last_raw", align_bytes=ALIGN, offset=0)
 
         def weave(s, e):
-            cols = slice(e % 2 * C, (e % 2 + 1) * C)
+            src, at, width = staged(s, e * C)
             nc.scalar.copy(
                 x_bf[e][:, s * C * PACK : (s + 1) * C * PACK].bitcast(F32).rearrange("p (c u) -> p c u", u=2),
-                picked[s][e // 2][:].bitcast(F32)[:, :, cols].rearrange("p u c -> p c u"),
+                src.bitcast(F32).rearrange("p (u c) -> p c u", u=2)[:, at : at + C, :],
             )
 
         def load_weights(e):
@@ -171,20 +184,20 @@ def tile_moe_loc_lin_gelu_kernel(tc, x_words, x_scales, xo, w, gate, offs, offs2
         gather_far(scale_rows, far_scale_win[:])
         gather_far(codes0, win0[:].bitcast(U32))
 
-        gather_row(2, 0, row2)
-        gather_row(2, 1, row2)
+        gather_row(2, 0, HALF, row2)
+        gather_row(2, HALF, HALF, row2)
+        round_row(row3, 3, [(T, round_on_gpsimd)], nc.sync)
         round_pairs(pair_a, 0, 0, HALF, whole, raw_pairs("raw_a1"))
         win1, codes1 = far_words(1)
-        gather_far(codes1, win1[:].bitcast(U32))
+        gather_far(codes1, win1[:].bitcast(U32), SLOTS - LATE)
         far_codes = [codes0, codes1]
-        round_row(row3, 3, [(T, round_on_gpsimd)], nc.sync)
-        round_pairs(pair_a, 0, 0, 0, shared, raw_pairs("raw_a0"))
+        round_pairs(pair_a, 0, 0, 0, [(C, round_on_gpsimd), (C, round_on_scalar)], raw_pairs("raw_a0"))
         gather_pairs(0, 0, pair_a)
-        gather_row(3, 0, planes[:, 0 : T + OVERLAP])
+        gather_row(3, 0, HALF, planes[:, 0 : T + OVERLAP])
         round_pairs(pair_b, 1, 0, HALF, whole, raw_pairs("raw_b1"))
         round_pairs(pair_b, 1, 0, 0, shared, raw_pairs("raw_b0"))
         gather_pairs(1, 0, pair_b)
-        gather_row(3, 1, planes[:, 0 : 3 * T + OVERLAP])
+        gather_row(3, HALF, HALF, planes[:, 0 : 3 * T + OVERLAP])
         round_pairs(pair_c, 1, 1, HALF, whole, raw_pairs("raw_c1"))
         round_pairs(pair_c, 1, 1, 0, shared, last_raw[:])
         gather_pairs(1, 1, pair_c)
@@ -232,10 +245,10 @@ def tile_moe_loc_lin_gelu_kernel(tc, x_words, x_scales, xo, w, gate, offs, offs2
 
         sums = {}
         banks = [psum.tile([N, 2, C], F32, name=f"bank{b}") for b in range(E + 1)]
-        far_sums = [banks[2][:, 1, :], banks[3][:, 1, :], banks[E][:, 0, :], banks[E][:, 1, :]]
+        far_sums = [banks[2][:, 1, :], banks[3][:, 1, :], banks[E][:, 0, :], banks[E][:, 1, 0 : C - LATE]]
 
         def multiply_far(e):
-            cols = slice(e * C, (e + 1) * C)
+            cols = slice(e * C, min((e + 1) * C, SLOTS - LATE))
             product(far_sums[e], e, lambda s: far_codes[s][:, cols], lambda s: far_scales[4 * s : P, cols])
 
         def multiply(e):
@@ -285,15 +298,26 @@ def tile_moe_loc_lin_gelu_kernel(tc, x_words, x_scales, xo, w, gate, offs, offs2
         multiply_far(1)
         multiply(3)
         give_back(2)
+        late_codes = tile([P, LATE], U32, "late_codes", tag="x_planes3")
+        nc.vector.tensor_copy(late_codes[:], win1[:].bitcast(U32).indirect(entries(far_list, SLOTS - LATE, LATE)))
         give_back(3)
         multiply_far(2)
         multiply_far(3)
+        late_sums = psum.tile([N, LATE], F32, name="late_sums")
+        late_cols = slice(SLOTS - LATE, SLOTS)
+        product(
+            late_sums[:], E - 1,
+            lambda s: late_codes[:] if s else far_codes[0][:, late_cols], lambda s: far_scales[4 * s : P, late_cols],
+        )
 
         first_act = tile([N, 2, C], F32, "far_act0", tag="x_codes3")
         for e in range(2):
             nc.scalar.activation(first_act[:, e, :], far_sums[e], GELU)
         nc.scalar.dma_start(out[:, T : T + HALF], first_act[:].rearrange("p i c -> p (i c)"))
         second_act = tile([N, HALF], F32, "far_act1")
-        nc.scalar.activation(second_act[:], banks[E][:].rearrange("p i c -> p (i c)"), GELU)
+        nc.scalar.activation(
+            second_act[:, 0 : HALF - LATE], banks[E][:].rearrange("p i c -> p (i c)")[:, 0 : HALF - LATE], GELU
+        )
+        nc.scalar.activation(second_act[:, HALF - LATE : HALF], late_sums[:], GELU)
         nc.scalar.dma_start(out[:, T + HALF : T + SLOTS], second_act[:])
         nc.sync.dma_start(out[:, 0:T], own_out[:])

@@ -28,6 +28,7 @@ ROW_SHARE = 640
 PAIR_SHARE = 320
 OVERLAP = 16
 LATE = 128
+WIDE = 1408
 
 
 def tile_moe_loc_lin_gelu_kernel(tc, x_words, x_scales, xo, w, gate, offs, offs2, out):
@@ -35,6 +36,7 @@ def tile_moe_loc_lin_gelu_kernel(tc, x_words, x_scales, xo, w, gate, offs, offs2
     with ExitStack() as ctx:
         keep = ctx.enter_context(tc.tile_pool(name="keep", bufs=1))
         reuse = ctx.enter_context(tc.tile_pool(name="reuse", bufs=1))
+        chain = ctx.enter_context(tc.tile_pool(name="chain", bufs=1))
         psum = ctx.enter_context(tc.psum_pool(name="psum", bufs=1))
 
         def tile(shape, dtype, name, tag=None):
@@ -49,22 +51,20 @@ def tile_moe_loc_lin_gelu_kernel(tc, x_words, x_scales, xo, w, gate, offs, offs2
         warm_in = keep.tile([P, 8], F32, name="warm_in")
         warm_out = keep.tile([P, 8], F32, name="warm_out")
 
-        far_scale_win = tile([P, Q], U8, "far_scale_win")
+        far_scale_win = tile([P, WIDE], U8, "far_scale_win")
         nc.vector.memset(warm_in[:], 0.0)
-        nc.vector.memset(far_scale_win[32:64, :].bitcast(I32), 0)
-        nc.vector.memset(far_scale_win[64:P, :].bitcast(I32), 0)
+        nc.vector.memset(far_scale_win[32:64, 0:Q].bitcast(I32), 0)
+        nc.vector.memset(far_scale_win[64:P, 0:Q].bitcast(I32), 0)
         far_scales = tile([P, SLOTS], U8, "far_scales")
         nc.vector.memset(far_scales[:].bitcast(I32), 0)
         nc.scalar.activation(warm_out[:], warm_in[:], GELU)
 
         def gather_far(dst, window, slots=SLOTS):
-            for first in range(0, slots, HALF):
-                count = min(HALF, slots - first)
-                nc.vector.tensor_copy(dst[:, first : first + count], window.indirect(entries(far_list, first, count)))
+            nc.vector.tensor_copy(dst[:, 0:slots], window.indirect(entries(far_list, 0, slots)))
 
         def far_words(s):
-            win = tile([P, Q], I32, f"far_word_win{s}")
-            nc.sync.dma_start(win[:], x_words[s].rearrange("p t d -> p (t d)").bitcast(I32))
+            win = tile([P, WIDE], I32, f"far_word_win{s}")
+            nc.sync.dma_start(win[:, 0:Q], x_words[s].rearrange("p t d -> p (t d)").bitcast(I32))
             codes = tile([P, SLOTS], U32, f"far_codes{s}")
             return win, codes
 
@@ -78,7 +78,10 @@ def tile_moe_loc_lin_gelu_kernel(tc, x_words, x_scales, xo, w, gate, offs, offs2
             return xo[s * K_PASS : (s + 1) * K_PASS, :].rearrange("(p j) t -> p j t", j=PACK)
 
         picked_early = tile([P, 4 * SLOTS], BF16, "picked0")
-        picked_late = [tile([P, 4 * HALF], BF16, f"picked1{h}") for h in range(2)]
+        def held(shape, dtype, name, stage, at=0):
+            return chain.tile(shape, dtype, name=name, align_bytes=ALIGN, offset=4096 * stage + at)
+
+        picked_late = [tile([P, 4 * HALF], BF16, "picked10"), held([P, 4 * HALF], BF16, "picked11", 0)]
 
         def staged(s, first):
             if s == 0:
@@ -123,9 +126,12 @@ def tile_moe_loc_lin_gelu_kernel(tc, x_words, x_scales, xo, w, gate, offs, offs2
             )
 
         woven = PASSES * C * PACK
-        x_early = reuse.tile([P, 3 * woven], BF16, name="x_early", align_bytes=ALIGN, offset=0)
-        x_bf = {e: x_early[:, e * woven : (e + 1) * woven] for e in range(3)}
-        last_raw = reuse.tile([P, 2, HALF], F32, name="last_raw", align_bytes=ALIGN, offset=0)
+        x_halves = [
+            reuse.tile([P, 2 * woven], BF16, name=f"x_half{h}", align_bytes=ALIGN, offset=4 * woven * h) for h in range(2)
+        ]
+        x_bf = {e: x_halves[e // 2][:, e % 2 * woven : (e % 2 + 1) * woven] for e in range(E)}
+        raw_b0 = reuse.tile([P, 2, HALF], F32, name="raw_b0", align_bytes=ALIGN, offset=0)
+        last_raw = reuse.tile([P, 2, HALF], F32, name="last_raw", align_bytes=ALIGN, offset=4 * woven)
 
         def weave(s, e):
             src, at, width = staged(s, e * C)
@@ -135,8 +141,8 @@ def tile_moe_loc_lin_gelu_kernel(tc, x_words, x_scales, xo, w, gate, offs, offs2
             )
 
         def load_weights(e):
-            if e == 2:
-                w_raw = reuse.tile([P, PASSES, PACK, N], F32, name="w_raw2", align_bytes=ALIGN, offset=12288)
+            if e >= 2:
+                w_raw = held([P, PASSES, PACK, N], F32, f"w_raw{e}", e - 1)
             else:
                 w_raw = tile([P, PASSES, PACK, N], F32, f"w_raw{e}")
             nc.sync.dma_start(w_raw[:], w[e].rearrange("(s p j) n -> p s j n", s=PASSES, j=PACK))
@@ -151,7 +157,10 @@ def tile_moe_loc_lin_gelu_kernel(tc, x_words, x_scales, xo, w, gate, offs, offs2
 
         def quantise_weights(e, passes_on_gpsimd):
             w_raw = w_raws[e]
-            w_bf = tile([P, PASSES, N, PACK], BF16, f"w_bf{e}")
+            if e >= 2:
+                w_bf = held([P, PASSES, N, PACK], BF16, f"w_bf{e}", e - 2, 1024)
+            else:
+                w_bf = tile([P, PASSES, N, PACK], BF16, f"w_bf{e}")
             if passes_on_gpsimd:
                 round_on_gpsimd(
                     w_bf[:, 0:passes_on_gpsimd, :, :], w_raw[:, 0:passes_on_gpsimd, :, :].rearrange("p s j n -> p s n j")
@@ -176,7 +185,7 @@ def tile_moe_loc_lin_gelu_kernel(tc, x_words, x_scales, xo, w, gate, offs, offs2
         shared = [(HALF - PAIR_SHARE, round_on_gpsimd), (PAIR_SHARE, round_on_scalar)]
 
         nc.sync.dma_start(far_list[:], offs2)
-        nc.sync.dma_start(far_scale_win[0:32, :].bitcast(I32), x_scales.rearrange("s b t -> (s b) t").bitcast(I32))
+        nc.sync.dma_start(far_scale_win[0:32, 0:Q].bitcast(I32), x_scales.rearrange("s b t -> (s b) t").bitcast(I32))
         round_row(row2, 2, [(ROW_SHARE, round_on_scalar), (T - ROW_SHARE, round_on_gpsimd)], nc.sync)
         nc.sync.dma_start(own_list[:], offs)
         win0, codes0 = far_words(0)
@@ -187,17 +196,19 @@ def tile_moe_loc_lin_gelu_kernel(tc, x_words, x_scales, xo, w, gate, offs, offs2
         gather_row(2, 0, HALF, row2)
         gather_row(2, HALF, HALF, row2)
         round_row(row3, 3, [(T, round_on_gpsimd)], nc.sync)
+        gather_row(3, 0, HALF, row3)
         round_pairs(pair_a, 0, 0, HALF, whole, raw_pairs("raw_a1"))
         win1, codes1 = far_words(1)
         gather_far(codes1, win1[:].bitcast(U32), SLOTS - LATE)
         far_codes = [codes0, codes1]
         round_pairs(pair_a, 0, 0, 0, [(C, round_on_gpsimd), (C, round_on_scalar)], raw_pairs("raw_a0"))
         gather_pairs(0, 0, pair_a)
-        gather_row(3, 0, HALF, planes[:, 0 : T + OVERLAP])
+        gather_row(3, HALF, HALF, planes[:, 0 : T + OVERLAP])
         round_pairs(pair_b, 1, 0, HALF, whole, raw_pairs("raw_b1"))
-        round_pairs(pair_b, 1, 0, 0, shared, raw_pairs("raw_b0"))
+        round_pairs(pair_b, 1, 0, 0, shared, raw_b0[:])
         gather_pairs(1, 0, pair_b)
-        gather_row(3, HALF, HALF, planes[:, 0 : 3 * T + OVERLAP])
+        for e in range(2):
+            weave(0, e)
         round_pairs(pair_c, 1, 1, HALF, whole, raw_pairs("raw_c1"))
         round_pairs(pair_c, 1, 1, 0, shared, last_raw[:])
         gather_pairs(1, 1, pair_c)
@@ -244,8 +255,9 @@ def tile_moe_loc_lin_gelu_kernel(tc, x_words, x_scales, xo, w, gate, offs, offs2
             tokens[e] = (x_codes, x_planes)
 
         sums = {}
-        banks = [psum.tile([N, 2, C], F32, name=f"bank{b}") for b in range(E + 1)]
-        far_sums = [banks[2][:, 1, :], banks[3][:, 1, :], banks[E][:, 0, :], banks[E][:, 1, 0 : C - LATE]]
+        banks = [psum.tile([N, C], F32, name=f"bank{b}") for b in range(E)]
+        far_banks = [psum.tile([N, 2, C], F32, name=f"far_bank{b}") for b in range(2)]
+        far_sums = [far_banks[0][:, 0, :], far_banks[0][:, 1, :], far_banks[1][:, 0, :], far_banks[1][:, 1, 0 : C - LATE]]
 
         def multiply_far(e):
             cols = slice(e * C, min((e + 1) * C, SLOTS - LATE))
@@ -253,17 +265,14 @@ def tile_moe_loc_lin_gelu_kernel(tc, x_words, x_scales, xo, w, gate, offs, offs2
 
         def multiply(e):
             x_codes, x_planes = tokens[e]
-            sums[e] = banks[e][:, 0, :]
+            sums[e] = banks[e][:]
             product(
                 sums[e], e,
                 lambda s: x_codes[:, s * C : (s + 1) * C], lambda s: x_planes[:, s * C : (s + 1) * C],
             )
 
         def give_back(e):
-            if e == 1:
-                act = reuse.tile([N, C], F32, name="act1", align_bytes=ALIGN, offset=12288)
-            else:
-                act = tile([N, C], F32, f"act{e}", tag="w_raw3" if e == 2 else None)
+            act = held([N, C], F32, f"act{e}", e) if e in (1, 2) else tile([N, C], F32, f"act{e}")
             nc.scalar.activation(act[:], sums[e], GELU)
             nc.vector.tensor_tensor(
                 own_out[:].indirect(entries(own_list, e * C, C)),
@@ -272,7 +281,12 @@ def tile_moe_loc_lin_gelu_kernel(tc, x_words, x_scales, xo, w, gate, offs, offs2
                 MULT,
             )
 
-        for e in range(3):
+        def hand_on(name, sums_in, first, count):
+            act = held([N, count], F32, name, 2, 1024) if first == 0 else tile([N, count], F32, name)
+            nc.scalar.activation(act[:], sums_in, GELU)
+            nc.scalar.dma_start(out[:, T + first : T + first + count], act[:])
+
+        for e in range(2, E):
             weave(0, e)
         for e in range(2):
             weave(1, e)
@@ -280,44 +294,32 @@ def tile_moe_loc_lin_gelu_kernel(tc, x_words, x_scales, xo, w, gate, offs, offs2
         quantise_tokens(0)
         multiply(0)
         quantise_tokens(1)
-        quantise_weights(1, 1)
+        for e in range(2, E):
+            weave(1, e)
+            quantise_tokens(e)
+        quantise_weights(1, 0)
         multiply(1)
-        weave(1, 2)
-        quantise_tokens(2)
         give_back(0)
         quantise_weights(2, 0)
-        multiply_far(0)
         multiply(2)
         give_back(1)
-        x_last = reuse.tile([P, woven], BF16, name="x_last", align_bytes=ALIGN, offset=12288 + 1024)
-        x_bf[3] = x_last[:]
-        for s in range(PASSES):
-            weave(s, 3)
-        quantise_tokens(3)
-        quantise_weights(3, 0)
+        multiply_far(0)
         multiply_far(1)
+        quantise_weights(3, 0)
         multiply(3)
         give_back(2)
+        hand_on("far_act0", far_banks[0][:].rearrange("p i c -> p (i c)"), 0, HALF)
         late_codes = tile([P, LATE], U32, "late_codes", tag="x_planes3")
-        nc.vector.tensor_copy(late_codes[:], win1[:].bitcast(U32).indirect(entries(far_list, SLOTS - LATE, LATE)))
+        nc.vector.tensor_copy(late_codes[:], win1[:, 0:Q].bitcast(U32).indirect(entries(far_list, SLOTS - LATE, LATE)))
         give_back(3)
         multiply_far(2)
         multiply_far(3)
+        hand_on("far_act1", far_banks[1][:].rearrange("p i c -> p (i c)")[:, 0 : HALF - LATE], HALF, HALF - LATE)
         late_sums = psum.tile([N, LATE], F32, name="late_sums")
         late_cols = slice(SLOTS - LATE, SLOTS)
         product(
             late_sums[:], E - 1,
             lambda s: late_codes[:] if s else far_codes[0][:, late_cols], lambda s: far_scales[4 * s : P, late_cols],
         )
-
-        first_act = tile([N, 2, C], F32, "far_act0", tag="x_codes3")
-        for e in range(2):
-            nc.scalar.activation(first_act[:, e, :], far_sums[e], GELU)
-        nc.scalar.dma_start(out[:, T : T + HALF], first_act[:].rearrange("p i c -> p (i c)"))
-        second_act = tile([N, HALF], F32, "far_act1")
-        nc.scalar.activation(
-            second_act[:, 0 : HALF - LATE], banks[E][:].rearrange("p i c -> p (i c)")[:, 0 : HALF - LATE], GELU
-        )
-        nc.scalar.activation(second_act[:, HALF - LATE : HALF], late_sums[:], GELU)
-        nc.scalar.dma_start(out[:, T + HALF : T + SLOTS], second_act[:])
+        hand_on("far_act2", late_sums[:], SLOTS - LATE, LATE)
         nc.sync.dma_start(out[:, 0:T], own_out[:])

@@ -25,7 +25,9 @@ SLOTS = E * C
 HALF = 512
 ALIGN = 256
 ROW_SHARE = 640
-PAIR_SHARE = 320
+FIRST = 448
+SECOND = T - FIRST
+PAIR_SHARE = 352
 OVERLAP = 16
 LATE = 128
 WIDE = 1408
@@ -79,17 +81,12 @@ def tile_moe_loc_lin_gelu_kernel(tc, x_words, x_scales, xo, w, gate, offs, offs2
 
         picked_early = tile([P, 4 * SLOTS], BF16, "picked0")
         def held(shape, dtype, name, stage, at=0):
-            return chain.tile(shape, dtype, name=name, align_bytes=ALIGN, offset=4096 * stage + at)
+            return chain.tile(shape, dtype, name=name, align_bytes=ALIGN, offset=8192 * stage + at)
 
-        picked_late = [tile([P, 4 * HALF], BF16, "picked10"), held([P, 4 * HALF], BF16, "picked11", 0)]
-
-        def staged(s, first):
-            if s == 0:
-                return picked_early[:], first, SLOTS
-            return picked_late[first // HALF][:], first % HALF, HALF
+        picked = [picked_early, held([P, 4 * SLOTS], BF16, "picked1", 0)]
 
         def round_pairs(pairs, s, u, first, shares, raw):
-            nc.sync.dma_start(raw, pass_rows(s)[:, 2 * u : 2 * u + 2, first : first + HALF])
+            nc.sync.dma_start(raw, pass_rows(s)[:, 2 * u : 2 * u + 2, first : first + raw.shape[2]])
             done = 0
             for count, rounder in shares:
                 rounder(
@@ -98,15 +95,14 @@ def tile_moe_loc_lin_gelu_kernel(tc, x_words, x_scales, xo, w, gate, offs, offs2
                 )
                 done += count
 
-        def raw_pairs(name):
-            return tile([P, 2, HALF], F32, name)[:]
+        def raw_pairs(name, count=HALF):
+            return tile([P, 2, count], F32, name)[:]
 
-        def gather_pairs(s, u, pairs):
-            for first in range(0, SLOTS, HALF):
-                dst, at, width = staged(s, first)
+        def gather_pairs(s, u, pairs, count):
+            for first in range(0, SLOTS, count):
                 nc.vector.tensor_copy(
-                    dst.bitcast(U32)[:, u * width + at : u * width + at + HALF],
-                    pairs.bitcast(U32).indirect(entries(own_list, first, HALF)),
+                    picked[s][:].bitcast(U32)[:, u * SLOTS + first : u * SLOTS + first + count],
+                    pairs.bitcast(U32).indirect(entries(own_list, first, count)),
                 )
 
         def round_row(row, j, shares, queue):
@@ -130,14 +126,13 @@ def tile_moe_loc_lin_gelu_kernel(tc, x_words, x_scales, xo, w, gate, offs, offs2
             reuse.tile([P, 2 * woven], BF16, name=f"x_half{h}", align_bytes=ALIGN, offset=4 * woven * h) for h in range(2)
         ]
         x_bf = {e: x_halves[e // 2][:, e % 2 * woven : (e % 2 + 1) * woven] for e in range(E)}
-        raw_b0 = reuse.tile([P, 2, HALF], F32, name="raw_b0", align_bytes=ALIGN, offset=0)
-        last_raw = reuse.tile([P, 2, HALF], F32, name="last_raw", align_bytes=ALIGN, offset=4 * woven)
+        raw_b0 = reuse.tile([P, 2, SECOND], F32, name="raw_b0", align_bytes=ALIGN, offset=0)
+        last_raw = reuse.tile([P, 2, SECOND], F32, name="last_raw", align_bytes=ALIGN, offset=4 * woven)
 
         def weave(s, e):
-            src, at, width = staged(s, e * C)
             nc.scalar.copy(
                 x_bf[e][:, s * C * PACK : (s + 1) * C * PACK].bitcast(F32).rearrange("p (c u) -> p c u", u=2),
-                src.bitcast(F32).rearrange("p (u c) -> p c u", u=2)[:, at : at + C, :],
+                picked[s][:].bitcast(F32).rearrange("p (u c) -> p c u", u=2)[:, e * C : (e + 1) * C, :],
             )
 
         def load_weights(e):
@@ -177,12 +172,13 @@ def tile_moe_loc_lin_gelu_kernel(tc, x_words, x_scales, xo, w, gate, offs, offs2
             )
             weights[e] = (w_codes, w_scales)
 
-        planes = tile([P, T + 2 * 2 * T], BF16, "planes")
-        row3, pair_a, pair_b = planes[:, 0:T], planes[:, T : 3 * T], planes[:, 3 * T : 5 * T]
+        planes = tile([P, T + 2 * WIDE], BF16, "planes")
+        row3, pair_a = planes[:, 0:T], planes[:, T : T + 2 * WIDE]
+        pair_b = tile([P, 2 * WIDE], BF16, "pair_b")[:]
         row2 = tile([P, T], BF16, "row2")[:]
         pair_c = tile([P, 2 * T], BF16, "pair_c")[:]
         whole = [(HALF, round_on_gpsimd)]
-        shared = [(HALF - PAIR_SHARE, round_on_gpsimd), (PAIR_SHARE, round_on_scalar)]
+        shared = [(SECOND - PAIR_SHARE, round_on_gpsimd), (PAIR_SHARE, round_on_scalar)]
 
         nc.sync.dma_start(far_list[:], offs2)
         nc.sync.dma_start(far_scale_win[0:32, 0:Q].bitcast(I32), x_scales.rearrange("s b t -> (s b) t").bitcast(I32))
@@ -202,16 +198,16 @@ def tile_moe_loc_lin_gelu_kernel(tc, x_words, x_scales, xo, w, gate, offs, offs2
         gather_far(codes1, win1[:].bitcast(U32), SLOTS - LATE)
         far_codes = [codes0, codes1]
         round_pairs(pair_a, 0, 0, 0, [(C, round_on_gpsimd), (C, round_on_scalar)], raw_pairs("raw_a0"))
-        gather_pairs(0, 0, pair_a)
+        gather_pairs(0, 0, pair_a[:, 0 : 2 * T], HALF)
         gather_row(3, HALF, HALF, planes[:, 0 : T + OVERLAP])
-        round_pairs(pair_b, 1, 0, HALF, whole, raw_pairs("raw_b1"))
+        round_pairs(pair_b, 1, 0, SECOND, [(FIRST, round_on_gpsimd)], raw_pairs("raw_b1", FIRST))
         round_pairs(pair_b, 1, 0, 0, shared, raw_b0[:])
-        gather_pairs(1, 0, pair_b)
+        gather_pairs(1, 0, pair_b, SLOTS)
         for e in range(2):
             weave(0, e)
-        round_pairs(pair_c, 1, 1, HALF, whole, raw_pairs("raw_c1"))
+        round_pairs(pair_c, 1, 1, SECOND, [(FIRST, round_on_gpsimd)], raw_pairs("raw_c1", FIRST))
         round_pairs(pair_c, 1, 1, 0, shared, last_raw[:])
-        gather_pairs(1, 1, pair_c)
+        gather_pairs(1, 1, pair_c, HALF)
 
         w_raws = [load_weights(e) for e in range(2)]
 

@@ -50,16 +50,17 @@ def tile_moe_loc_lin_gelu_kernel(tc, x_words, x_scales, xo, w, gate, offs, offs2
         own_list = keep.tile([P, SLOTS // 16], U16, name="own_list")
         far_list = keep.tile([P, SLOTS // 16], U16, name="far_list")
 
-        warm_in = keep.tile([P, 8], F32, name="warm_in")
-        warm_out = keep.tile([P, 8], F32, name="warm_out")
+        zero = keep.tile([P, 8], F32, name="zero")
 
         far_scale_win = tile([P, WIDE], U8, "far_scale_win")
-        nc.vector.memset(warm_in[:], 0.0)
+        nc.vector.memset(zero[:], 0.0)
         nc.vector.memset(far_scale_win[32:64, 0:Q].bitcast(I32), 0)
         nc.vector.memset(far_scale_win[64:P, 0:Q].bitcast(I32), 0)
         far_scales = tile([P, SLOTS], U8, "far_scales")
         nc.vector.memset(far_scales[:].bitcast(I32), 0)
-        nc.scalar.activation(warm_out[:], warm_in[:], GELU)
+        windows = [tile([P, T], F32, f"window{i}") for i in range(2)]
+        nc.scalar.activation(windows[0][:], zero[:, 0:1].to_broadcast([P, T]), GELU)
+        nc.vector.memset(windows[1][:].bitcast(I32), 0)
 
         def gather_far(dst, window, slots=SLOTS):
             nc.vector.tensor_copy(dst[:, 0:slots], window.indirect(entries(far_list, 0, slots)))
@@ -79,11 +80,11 @@ def tile_moe_loc_lin_gelu_kernel(tc, x_words, x_scales, xo, w, gate, offs, offs2
         def pass_rows(s):
             return xo[s * K_PASS : (s + 1) * K_PASS, :].rearrange("(p j) t -> p j t", j=PACK)
 
-        picked_early = tile([P, 4 * SLOTS], BF16, "picked0")
         def held(shape, dtype, name, stage, at=0):
             return chain.tile(shape, dtype, name=name, align_bytes=ALIGN, offset=8192 * stage + at)
 
-        picked = [picked_early, held([P, 4 * SLOTS], BF16, "picked1", 0)]
+        picked_early = tile([P, 4 * SLOTS], BF16, "picked0")
+        picked = [picked_early, tile([P, 4 * SLOTS], BF16, "picked1")]
 
         def round_pairs(pairs, s, u, first, shares, raw):
             nc.sync.dma_start(raw, pass_rows(s)[:, 2 * u : 2 * u + 2, first : first + raw.shape[2]])
@@ -129,10 +130,10 @@ def tile_moe_loc_lin_gelu_kernel(tc, x_words, x_scales, xo, w, gate, offs, offs2
         raw_b0 = reuse.tile([P, 2, SECOND], F32, name="raw_b0", align_bytes=ALIGN, offset=0)
         last_raw = reuse.tile([P, 2, SECOND], F32, name="last_raw", align_bytes=ALIGN, offset=4 * woven)
 
-        def weave(s, e):
-            nc.scalar.copy(
-                x_bf[e][:, s * C * PACK : (s + 1) * C * PACK].bitcast(F32).rearrange("p (c u) -> p c u", u=2),
-                picked[s][:].bitcast(F32).rearrange("p (u c) -> p c u", u=2)[:, e * C : (e + 1) * C, :],
+        def weave(s, e, copy=nc.scalar.copy, word=F32, dst=None):
+            copy(
+                (x_bf[e][:, s * C * PACK : (s + 1) * C * PACK] if dst is None else dst).bitcast(word).rearrange("p (c u) -> p c u", u=2),
+                picked[s][:].bitcast(word).rearrange("p (u c) -> p c u", u=2)[:, e * C : (e + 1) * C, :],
             )
 
         def load_weights(e):
@@ -150,12 +151,11 @@ def tile_moe_loc_lin_gelu_kernel(tc, x_words, x_scales, xo, w, gate, offs, offs2
 
         weights = {}
 
-        def quantise_weights(e, passes_on_gpsimd):
+        w_bfs = {}
+
+        def round_weights(e, passes_on_gpsimd):
             w_raw = w_raws[e]
-            if e >= 2:
-                w_bf = held([P, PASSES, N, PACK], BF16, f"w_bf{e}", e - 2, 1024)
-            else:
-                w_bf = tile([P, PASSES, N, PACK], BF16, f"w_bf{e}")
+            w_bf = held([P, PASSES, N, PACK], BF16, f"w_bf{e}", e // 3, 4096 if e == 1 else 1024)
             if passes_on_gpsimd:
                 round_on_gpsimd(
                     w_bf[:, 0:passes_on_gpsimd, :, :], w_raw[:, 0:passes_on_gpsimd, :, :].rearrange("p s j n -> p s n j")
@@ -165,6 +165,10 @@ def tile_moe_loc_lin_gelu_kernel(tc, x_words, x_scales, xo, w, gate, offs, offs2
                     w_bf[:, s, :, :].rearrange("p (c i) j -> p c j i", i=4),
                     w_raw[:, s, :, :].rearrange("p j (c i) -> p c j i", i=4),
                 )
+            w_bfs[e] = w_bf
+
+        def quantise_weights(e):
+            w_bf = w_bfs[e]
             w_codes = tile([P, PASSES * N], U32, f"w_codes{e}")
             w_scales = tile([P, PASSES * N], U8, f"w_scales{e}")
             nc.vector.quantize_mx(
@@ -225,8 +229,6 @@ def tile_moe_loc_lin_gelu_kernel(tc, x_words, x_scales, xo, w, gate, offs, offs2
         w_raws.append(load_weights(3))
         gates.append(load_gate(1))
 
-        own_out = tile([P, T], F32, "own_out")
-
         def product(acc, e, codes, scales):
             w_codes, w_scales = weights[e]
             for s in range(PASSES):
@@ -242,12 +244,14 @@ def tile_moe_loc_lin_gelu_kernel(tc, x_words, x_scales, xo, w, gate, offs, offs2
 
         tokens = {}
 
-        def quantise_tokens(e):
+        def quantise_tokens(e, second=None):
             x_codes = tile([P, PASSES * C], U32, f"x_codes{e}")
             x_planes = tile([P, PASSES * C], U8, f"x_planes{e}")
-            nc.vector.quantize_mx(
-                out=x_codes[:].bitcast(FP8X4), scales=x_planes[:], in_=x_bf[e]
-            )
+            parts = [x_bf[e]] if second is None else [x_bf[e][:, 0 : C * PACK], second]
+            width = PASSES * C // len(parts)
+            for i, part in enumerate(parts):
+                cols = slice(i * width, (i + 1) * width)
+                nc.vector.quantize_mx(out=x_codes[:, cols].bitcast(FP8X4), scales=x_planes[:, cols], in_=part)
             tokens[e] = (x_codes, x_planes)
 
         sums = {}
@@ -267,55 +271,70 @@ def tile_moe_loc_lin_gelu_kernel(tc, x_words, x_scales, xo, w, gate, offs, offs2
                 lambda s: x_codes[:, s * C : (s + 1) * C], lambda s: x_planes[:, s * C : (s + 1) * C],
             )
 
-        def give_back(e):
-            act = held([N, C], F32, f"act{e}", e) if e in (1, 2) else tile([N, C], F32, f"act{e}")
-            nc.scalar.activation(act[:], sums[e], GELU)
-            nc.vector.tensor_tensor(
-                own_out[:].indirect(entries(own_list, e * C, C)),
-                act[:],
-                gates[e // 2][:, e % 2 * C : (e % 2 + 1) * C],
-                MULT,
-            )
+        acts = {}
+
+        def activate(e):
+            acts[e] = held([N, C], F32, f"act{e}", 2, 1024 * e) if e < 3 else tile([N, C], F32, f"act{e}")
+            nc.scalar.activation(acts[e][:], sums[e], GELU)
+
+        def gate_of(e):
+            return gates[e // 2][:, e % 2 * C : (e % 2 + 1) * C]
+
+        def places(e):
+            return windows[e // 2][:].indirect(entries(own_list, e * C, C))
+
+        def weigh(e):
+            gated = held([N, C], F32, f"gated{e}", 3, 1024 * e)
+            nc.vector.tensor_tensor(gated[:], acts[e][:], gate_of(e), MULT)
+            acts[e] = gated
 
         def hand_on(name, sums_in, first, count):
-            act = held([N, count], F32, name, 2, 1024) if first == 0 else tile([N, count], F32, name)
+            act = held([N, count], F32, name, 2, 3072) if first == 0 else held([N, count], F32, name, 3, 1024)
             nc.scalar.activation(act[:], sums_in, GELU)
-            nc.scalar.dma_start(out[:, T + first : T + first + count], act[:])
+            nc.sync.dma_start(out[:, T + first : T + first + count], act[:])
 
         for e in range(2, E):
             weave(0, e)
+        for e in range(3):
+            weave(1, e)
         for e in range(2):
-            weave(1, e)
-        quantise_weights(0, 2)
-        quantise_tokens(0)
-        multiply(0)
-        quantise_tokens(1)
-        for e in range(2, E):
-            weave(1, e)
+            round_weights(e, PASSES)
+            quantise_weights(e)
             quantise_tokens(e)
-        quantise_weights(1, 0)
-        multiply(1)
-        give_back(0)
-        quantise_weights(2, 0)
-        multiply(2)
-        give_back(1)
+            multiply(e)
+        last_woven = held([P, C * PACK], BF16, "last_woven", 0, 4096)[:]
+        weave(1, 3, nc.vector.tensor_copy, I32, last_woven)
         multiply_far(0)
         multiply_far(1)
-        quantise_weights(3, 0)
-        multiply(3)
-        give_back(2)
-        hand_on("far_act0", far_banks[0][:].rearrange("p i c -> p (i c)"), 0, HALF)
+        quantise_tokens(2)
+        quantise_tokens(3, last_woven)
+        for e in range(2, E):
+            round_weights(e, 0)
+            quantise_weights(e)
+            multiply(e)
         late_codes = tile([P, LATE], U32, "late_codes", tag="x_planes3")
         nc.vector.tensor_copy(late_codes[:], win1[:, 0:Q].bitcast(U32).indirect(entries(far_list, SLOTS - LATE, LATE)))
-        give_back(3)
         multiply_far(2)
         multiply_far(3)
-        hand_on("far_act1", far_banks[1][:].rearrange("p i c -> p (i c)")[:, 0 : HALF - LATE], HALF, HALF - LATE)
-        late_sums = psum.tile([N, LATE], F32, name="late_sums")
+        late_sums = far_banks[1][:, 1, C - LATE : C]
         late_cols = slice(SLOTS - LATE, SLOTS)
         product(
-            late_sums[:], E - 1,
+            late_sums, E - 1,
             lambda s: late_codes[:] if s else far_codes[0][:, late_cols], lambda s: far_scales[4 * s : P, late_cols],
         )
-        hand_on("far_act2", late_sums[:], SLOTS - LATE, LATE)
-        nc.sync.dma_start(out[:, 0:T], own_out[:])
+        for e in range(3):
+            activate(e)
+        hand_on("far_act0", far_banks[0][:].rearrange("p i c -> p (i c)"), 0, HALF)
+        for e in range(2):
+            weigh(e)
+        nc.scalar.activation(places(0), acts[0][:], COPY)
+        activate(3)
+        nc.scalar.activation(places(1), acts[1][:], COPY)
+        for e in range(2, E):
+            nc.vector.tensor_tensor(places(e), acts[e][:], gate_of(e), MULT)
+        hand_on("far_act1", far_banks[1][:].rearrange("p i c -> p (i c)"), HALF, HALF)
+        for h in range(2):
+            cols = slice(h * HALF, (h + 1) * HALF)
+            own = tile([P, HALF], F32, f"own{h}")
+            nc.vector.tensor_tensor(own[:], windows[0][:, cols], windows[1][:, cols], ADD)
+            nc.sync.dma_start(out[:, cols], own[:])

@@ -29,7 +29,8 @@ FIRST = 448
 SECOND = T - FIRST
 PAIR_SHARE = 352
 OVERLAP = 16
-LATE = 128
+LATE = 256
+SPLIT = 448
 WIDE = 1408
 
 
@@ -83,7 +84,7 @@ def tile_moe_loc_lin_gelu_kernel(tc, x_words, x_scales, xo, w, gate, offs, offs2
         def held(shape, dtype, name, stage, at=0):
             return chain.tile(shape, dtype, name=name, align_bytes=ALIGN, offset=8192 * stage + at)
 
-        picked_early = tile([P, 4 * SLOTS], BF16, "picked0")
+        picked_early = held([P, 4 * SLOTS], BF16, "picked0", 4)
         picked = [picked_early, tile([P, 4 * SLOTS], BF16, "picked1")]
 
         def round_pairs(pairs, s, u, first, shares, raw):
@@ -130,24 +131,19 @@ def tile_moe_loc_lin_gelu_kernel(tc, x_words, x_scales, xo, w, gate, offs, offs2
         raw_b0 = reuse.tile([P, 2, SECOND], F32, name="raw_b0", align_bytes=ALIGN, offset=0)
         last_raw = reuse.tile([P, 2, SECOND], F32, name="last_raw", align_bytes=ALIGN, offset=4 * woven)
 
-        def weave(s, e, copy=nc.scalar.copy, word=F32, dst=None):
-            copy(
-                (x_bf[e][:, s * C * PACK : (s + 1) * C * PACK] if dst is None else dst).bitcast(word).rearrange("p (c u) -> p c u", u=2),
-                picked[s][:].bitcast(word).rearrange("p (u c) -> p c u", u=2)[:, e * C : (e + 1) * C, :],
+        def weave(s, e):
+            nc.scalar.copy(
+                x_bf[e][:, s * C * PACK : (s + 1) * C * PACK].bitcast(F32).rearrange("p (c u) -> p c u", u=2),
+                picked[s][:].bitcast(F32).rearrange("p (u c) -> p c u", u=2)[:, e * C : (e + 1) * C, :],
             )
 
         def load_weights(e):
-            if e >= 2:
-                w_raw = held([P, PASSES, PACK, N], F32, f"w_raw{e}", e - 1)
+            if e == 2:
+                w_raw = held([P, PASSES, PACK, N], F32, f"w_raw{e}", 1)
             else:
                 w_raw = tile([P, PASSES, PACK, N], F32, f"w_raw{e}")
             nc.sync.dma_start(w_raw[:], w[e].rearrange("(s p j) n -> p s j n", s=PASSES, j=PACK))
             return w_raw
-
-        def load_gate(h):
-            part = tile([P, HALF], F32, f"gate{h}")
-            nc.sync.dma_start(part[:], gate[:, h * HALF : (h + 1) * HALF])
-            return part
 
         weights = {}
 
@@ -155,7 +151,7 @@ def tile_moe_loc_lin_gelu_kernel(tc, x_words, x_scales, xo, w, gate, offs, offs2
 
         def round_weights(e, passes_on_gpsimd):
             w_raw = w_raws[e]
-            w_bf = held([P, PASSES, N, PACK], BF16, f"w_bf{e}", e // 3, 4096 if e == 1 else 1024)
+            w_bf = held([P, PASSES, N, PACK], BF16, f"w_bf{e}", 0, (3072, 6144, 2048, 4096)[e])
             if passes_on_gpsimd:
                 round_on_gpsimd(
                     w_bf[:, 0:passes_on_gpsimd, :, :], w_raw[:, 0:passes_on_gpsimd, :, :].rearrange("p s j n -> p s n j")
@@ -207,6 +203,14 @@ def tile_moe_loc_lin_gelu_kernel(tc, x_words, x_scales, xo, w, gate, offs, offs2
         round_pairs(pair_b, 1, 0, SECOND, [(FIRST, round_on_gpsimd)], raw_pairs("raw_b1", FIRST))
         round_pairs(pair_b, 1, 0, 0, shared, raw_b0[:])
         gather_pairs(1, 0, pair_b, SLOTS)
+
+        def place_scale_rows(blocks):
+            for block in blocks:
+                s, quad = divmod(block, 4)
+                to, src = 32 * quad + 4 * s, 4 * block
+                nc.sync.dma_start(far_scales[to : to + 4, :].bitcast(I32), scale_rows[src : src + 4, :].bitcast(I32))
+
+        place_scale_rows(range(0, 4))
         for e in range(2):
             weave(0, e)
         round_pairs(pair_c, 1, 1, SECOND, [(FIRST, round_on_gpsimd)], raw_pairs("raw_c1", FIRST))
@@ -215,19 +219,10 @@ def tile_moe_loc_lin_gelu_kernel(tc, x_words, x_scales, xo, w, gate, offs, offs2
 
         w_raws = [load_weights(e) for e in range(2)]
 
-        def place_scale_rows(blocks):
-            for block in blocks:
-                s, quad = divmod(block, 4)
-                to, src = 32 * quad + 4 * s, 4 * block
-                nc.sync.dma_start(far_scales[to : to + 4, :].bitcast(I32), scale_rows[src : src + 4, :].bitcast(I32))
-
-        place_scale_rows(range(0, 3))
-        gates = [load_gate(0)]
-        place_scale_rows(range(3, 6))
-        w_raws.append(load_weights(2))
-        place_scale_rows(range(6, 8))
-        w_raws.append(load_weights(3))
-        gates.append(load_gate(1))
+        place_scale_rows(range(4, 8))
+        w_raws.extend(load_weights(e) for e in range(2, E))
+        gates = tile([P, SLOTS], F32, "gates")
+        nc.sync.dma_start(gates[:], gate)
 
         def product(acc, e, codes, scales):
             w_codes, w_scales = weights[e]
@@ -244,24 +239,26 @@ def tile_moe_loc_lin_gelu_kernel(tc, x_words, x_scales, xo, w, gate, offs, offs2
 
         tokens = {}
 
-        def quantise_tokens(e, second=None):
-            x_codes = tile([P, PASSES * C], U32, f"x_codes{e}")
+        def quantise_tokens(e):
+            if e == E - 1:
+                x_codes = held([P, PASSES * C], U32, f"x_codes{e}", 2)
+            else:
+                x_codes = tile([P, PASSES * C], U32, f"x_codes{e}")
             x_planes = tile([P, PASSES * C], U8, f"x_planes{e}")
-            parts = [x_bf[e]] if second is None else [x_bf[e][:, 0 : C * PACK], second]
-            width = PASSES * C // len(parts)
-            for i, part in enumerate(parts):
-                cols = slice(i * width, (i + 1) * width)
-                nc.vector.quantize_mx(out=x_codes[:, cols].bitcast(FP8X4), scales=x_planes[:, cols], in_=part)
+            nc.vector.quantize_mx(out=x_codes[:].bitcast(FP8X4), scales=x_planes[:], in_=x_bf[e])
             tokens[e] = (x_codes, x_planes)
 
         sums = {}
         banks = [psum.tile([N, C], F32, name=f"bank{b}") for b in range(E)]
         far_banks = [psum.tile([N, 2, C], F32, name=f"far_bank{b}") for b in range(2)]
-        far_sums = [far_banks[0][:, 0, :], far_banks[0][:, 1, :], far_banks[1][:, 0, :], far_banks[1][:, 1, 0 : C - LATE]]
 
         def multiply_far(e):
-            cols = slice(e * C, min((e + 1) * C, SLOTS - LATE))
-            product(far_sums[e], e, lambda s: far_codes[s][:, cols], lambda s: far_scales[4 * s : P, cols])
+            cols = slice(e * C, (e + 1) * C)
+            second = late_codes[:] if e == E - 1 else far_codes[1][:, cols]
+            product(
+                far_banks[e // 2][:, e % 2, :], e,
+                lambda s: second if s else far_codes[0][:, cols], lambda s: far_scales[4 * s : P, cols],
+            )
 
         def multiply(e):
             x_codes, x_planes = tokens[e]
@@ -271,68 +268,61 @@ def tile_moe_loc_lin_gelu_kernel(tc, x_words, x_scales, xo, w, gate, offs, offs2
                 lambda s: x_codes[:, s * C : (s + 1) * C], lambda s: x_planes[:, s * C : (s + 1) * C],
             )
 
-        acts = {}
+        def activate(act, sums_in):
+            nc.scalar.activation(act, sums_in, GELU)
 
-        def activate(e):
-            acts[e] = held([N, C], F32, f"act{e}", 2, 1024 * e) if e < 3 else tile([N, C], F32, f"act{e}")
-            nc.scalar.activation(acts[e][:], sums[e], GELU)
+        def places(window, first, last):
+            return windows[window][:].indirect(entries(own_list, first, last - first))
 
-        def gate_of(e):
-            return gates[e // 2][:, e % 2 * C : (e % 2 + 1) * C]
+        def weigh(e, act, count):
+            gated = held([N, count], F32, f"gated{e}", 3, 1024 * e)
+            nc.vector.tensor_tensor(gated[:], act[:, 0:count], gates[:, e * C : e * C + count], MULT)
+            return gated[:]
 
-        def places(e):
-            return windows[e // 2][:].indirect(entries(own_list, e * C, C))
-
-        def weigh(e):
-            gated = held([N, C], F32, f"gated{e}", 3, 1024 * e)
-            nc.vector.tensor_tensor(gated[:], acts[e][:], gate_of(e), MULT)
-            acts[e] = gated
-
-        def hand_on(name, sums_in, first, count):
-            act = held([N, count], F32, name, 2, 3072) if first == 0 else held([N, count], F32, name, 3, 1024)
-            nc.scalar.activation(act[:], sums_in, GELU)
-            nc.sync.dma_start(out[:, T + first : T + first + count], act[:])
+        def hand_on(act, sums_in, first):
+            nc.scalar.activation(act, sums_in, GELU)
+            nc.sync.dma_start(out[:, T + first : T + first + act.shape[1]], act)
 
         for e in range(2, E):
             weave(0, e)
-        for e in range(3):
+        late_codes = held([P, LATE], U32, "late_codes", 4)
+        nc.vector.tensor_copy(late_codes[:], win1[:, 0:Q].bitcast(U32).indirect(entries(far_list, SLOTS - LATE, LATE)))
+        for e in range(E):
             weave(1, e)
         for e in range(2):
             round_weights(e, PASSES)
             quantise_weights(e)
             quantise_tokens(e)
             multiply(e)
-        last_woven = held([P, C * PACK], BF16, "last_woven", 0, 4096)[:]
-        weave(1, 3, nc.vector.tensor_copy, I32, last_woven)
         multiply_far(0)
         multiply_far(1)
         quantise_tokens(2)
-        quantise_tokens(3, last_woven)
-        for e in range(2, E):
-            round_weights(e, 0)
-            quantise_weights(e)
-            multiply(e)
-        late_codes = tile([P, LATE], U32, "late_codes", tag="x_planes3")
-        nc.vector.tensor_copy(late_codes[:], win1[:, 0:Q].bitcast(U32).indirect(entries(far_list, SLOTS - LATE, LATE)))
+        quantise_tokens(3)
+        round_weights(2, 0)
+        quantise_weights(2)
+        multiply(2)
+        early = [held([N, C], F32, f"act{e}", 1, 2048 * e) for e in range(2)]
+        activate(early[0][:], sums[0])
+        activate(early[1][:, 0 : SPLIT - C], sums[1][:, 0 : SPLIT - C])
+        gated = [weigh(0, early[0], C), weigh(1, early[1], SPLIT - C)]
+        round_weights(3, 0)
+        quantise_weights(3)
+        multiply(3)
         multiply_far(2)
         multiply_far(3)
-        late_sums = far_banks[1][:, 1, C - LATE : C]
-        late_cols = slice(SLOTS - LATE, SLOTS)
-        product(
-            late_sums, E - 1,
-            lambda s: late_codes[:] if s else far_codes[0][:, late_cols], lambda s: far_scales[4 * s : P, late_cols],
-        )
-        for e in range(3):
-            activate(e)
-        hand_on("far_act0", far_banks[0][:].rearrange("p i c -> p (i c)"), 0, HALF)
-        for e in range(2):
-            weigh(e)
-        nc.scalar.activation(places(0), acts[0][:], COPY)
-        activate(3)
-        nc.scalar.activation(places(1), acts[1][:], COPY)
-        for e in range(2, E):
-            nc.vector.tensor_tensor(places(e), acts[e][:], gate_of(e), MULT)
-        hand_on("far_act1", far_banks[1][:].rearrange("p i c -> p (i c)"), HALF, HALF)
+        middle = held([N, 3 * C - SPLIT], F32, "middle", 1)
+        activate(middle[:, 0 : 2 * C - SPLIT], sums[1][:, SPLIT - C : C])
+        activate(middle[:, 2 * C - SPLIT : 3 * C - SPLIT], sums[2])
+        nc.scalar.activation(places(0, 0, C), gated[0], COPY)
+        last_act = tile([N, C], F32, "act3")
+        activate(last_act[:], sums[3])
+        far_acts = held([N, 3 * C], F32, "far_acts", 2)
+        hand_on(far_acts[:, 0:HALF], far_banks[0][:].rearrange("p i c -> p (i c)"), 0)
+        hand_on(far_acts[:, HALF : 3 * C], far_banks[1][:, 0, :], HALF)
+        nc.scalar.activation(places(0, C, SPLIT), gated[1], COPY)
+        nc.vector.tensor_tensor(places(1, SPLIT, 3 * C), middle[:], gates[:, SPLIT : 3 * C], MULT)
+        nc.vector.tensor_tensor(places(1, 3 * C, SLOTS), last_act[:], gates[:, 3 * C : SLOTS], MULT)
+        hand_on(held([N, C], F32, "far_act3", 3, 1024)[:], far_banks[1][:, 1, :], 3 * C)
         for h in range(2):
             cols = slice(h * HALF, (h + 1) * HALF)
             own = tile([P, HALF], F32, f"own{h}")

@@ -137,9 +137,21 @@ def tile_moe_loc_lin_gelu_kernel(tc, x_words, x_scales, xo, w, gate, offs, offs2
                 picked[s][:].bitcast(F32).rearrange("p (u c) -> p c u", u=2)[:, e * C : (e + 1) * C, :],
             )
 
+        def weave_half(s, h):
+            nc.scalar.copy(
+                x_halves[h][:].bitcast(F32).rearrange("p (e s c u) -> p s e c u", e=2, s=PASSES, u=2)[:, s],
+                picked[s][:].bitcast(F32).rearrange("p (u h e c) -> p h e c u", u=2, h=2, e=2)[:, h],
+            )
+
         def load_weights(e):
+            if e == E - 1:
+                parts = [held([P, PACK, N], F32, "w_raw3_0", 1, 1024), tile([P, PACK, N], F32, "w_raw3_1")]
+                for s in range(PASSES):
+                    rows = w[e, s * K_PASS : (s + 1) * K_PASS, :]
+                    nc.sync.dma_start(parts[s][:], rows.rearrange("(p j) n -> p j n", j=PACK))
+                return parts
             if e == 2:
-                w_raw = held([P, PASSES, PACK, N], F32, f"w_raw{e}", 1)
+                w_raw = held([P, PASSES, PACK, N], F32, f"w_raw{e}", 2)
             else:
                 w_raw = tile([P, PASSES, PACK, N], F32, f"w_raw{e}")
             nc.sync.dma_start(w_raw[:], w[e].rearrange("(s p j) n -> p s j n", s=PASSES, j=PACK))
@@ -156,10 +168,15 @@ def tile_moe_loc_lin_gelu_kernel(tc, x_words, x_scales, xo, w, gate, offs, offs2
                 round_on_gpsimd(
                     w_bf[:, 0:passes_on_gpsimd, :, :], w_raw[:, 0:passes_on_gpsimd, :, :].rearrange("p s j n -> p s n j")
                 )
-            for s in range(passes_on_gpsimd, PASSES):
+            elif e == E - 1:
+                for s in range(PASSES):
+                    round_on_scalar(
+                        w_bf[:, s, :, :].rearrange("p (c i) j -> p c j i", i=4),
+                        w_raw[s][:].rearrange("p j (c i) -> p c j i", i=4),
+                    )
+            else:
                 round_on_scalar(
-                    w_bf[:, s, :, :].rearrange("p (c i) j -> p c j i", i=4),
-                    w_raw[:, s, :, :].rearrange("p j (c i) -> p c j i", i=4),
+                    w_bf[:].rearrange("p s (c i) j -> p s c j i", i=4), w_raw[:].rearrange("p s j (c i) -> p s c j i", i=4)
                 )
             w_bfs[e] = w_bf
 
@@ -210,6 +227,7 @@ def tile_moe_loc_lin_gelu_kernel(tc, x_words, x_scales, xo, w, gate, offs, offs2
                 to, src = 32 * quad + 4 * s, 4 * block
                 nc.sync.dma_start(far_scales[to : to + 4, :].bitcast(I32), scale_rows[src : src + 4, :].bitcast(I32))
 
+
         place_scale_rows(range(0, 4))
         for e in range(2):
             weave(0, e)
@@ -218,7 +236,6 @@ def tile_moe_loc_lin_gelu_kernel(tc, x_words, x_scales, xo, w, gate, offs, offs2
         gather_pairs(1, 1, pair_c, HALF)
 
         w_raws = [load_weights(e) for e in range(2)]
-
         place_scale_rows(range(4, 8))
         w_raws.extend(load_weights(e) for e in range(2, E))
         gates = tile([P, SLOTS], F32, "gates")
@@ -249,8 +266,9 @@ def tile_moe_loc_lin_gelu_kernel(tc, x_words, x_scales, xo, w, gate, offs, offs2
             tokens[e] = (x_codes, x_planes)
 
         sums = {}
-        banks = [psum.tile([N, C], F32, name=f"bank{b}") for b in range(E)]
-        far_banks = [psum.tile([N, 2, C], F32, name=f"far_bank{b}") for b in range(2)]
+        early_bank = psum.tile([N, 2 * C], F32, name="early_bank", tag="shared_bank")
+        banks = [early_bank[:, 0:C], early_bank[:, C : 2 * C]] + [psum.tile([N, C], F32, name=f"bank{b}") for b in (2, 3)]
+        far_banks = []
 
         def multiply_far(e):
             cols = slice(e * C, (e + 1) * C)
@@ -274,52 +292,47 @@ def tile_moe_loc_lin_gelu_kernel(tc, x_words, x_scales, xo, w, gate, offs, offs2
         def places(window, first, last):
             return windows[window][:].indirect(entries(own_list, first, last - first))
 
-        def weigh(e, act, count):
-            gated = held([N, count], F32, f"gated{e}", 3, 1024 * e)
-            nc.vector.tensor_tensor(gated[:], act[:, 0:count], gates[:, e * C : e * C + count], MULT)
-            return gated[:]
-
         def hand_on(act, sums_in, first):
             nc.scalar.activation(act, sums_in, GELU)
             nc.sync.dma_start(out[:, T + first : T + first + act.shape[1]], act)
 
-        for e in range(2, E):
-            weave(0, e)
+        weave_half(0, 1)
         late_codes = held([P, LATE], U32, "late_codes", 4)
         nc.vector.tensor_copy(late_codes[:], win1[:, 0:Q].bitcast(U32).indirect(entries(far_list, SLOTS - LATE, LATE)))
-        for e in range(E):
+        for e in range(2):
             weave(1, e)
+        weave_half(1, 1)
         for e in range(2):
             round_weights(e, PASSES)
             quantise_weights(e)
             quantise_tokens(e)
             multiply(e)
-        multiply_far(0)
-        multiply_far(1)
         quantise_tokens(2)
-        quantise_tokens(3)
         round_weights(2, 0)
         quantise_weights(2)
         multiply(2)
-        early = [held([N, C], F32, f"act{e}", 1, 2048 * e) for e in range(2)]
-        activate(early[0][:], sums[0])
-        activate(early[1][:, 0 : SPLIT - C], sums[1][:, 0 : SPLIT - C])
-        gated = [weigh(0, early[0], C), weigh(1, early[1], SPLIT - C)]
+        quantise_tokens(3)
         round_weights(3, 0)
         quantise_weights(3)
         multiply(3)
-        multiply_far(2)
-        multiply_far(3)
-        middle = held([N, 3 * C - SPLIT], F32, "middle", 1)
+        early = held([N, SPLIT], F32, "early_acts", 1)
+        activate(early[:], early_bank[:, 0:SPLIT])
+        gated = held([N, SPLIT], F32, "gated", 3)
+        nc.vector.tensor_tensor(gated[:], early[:], gates[:, 0:SPLIT], MULT)
+        middle = held([N, 3 * C - SPLIT], F32, "middle", 1, 2048)
         activate(middle[:, 0 : 2 * C - SPLIT], sums[1][:, SPLIT - C : C])
         activate(middle[:, 2 * C - SPLIT : 3 * C - SPLIT], sums[2])
-        nc.scalar.activation(places(0, 0, C), gated[0], COPY)
+        far_banks.append(psum.tile([N, 2, C], F32, name="far_bank0", tag="shared_bank"))
+        far_banks.append(psum.tile([N, 2, C], F32, name="far_bank1"))
+        for e in range(E):
+            multiply_far(e)
+        nc.scalar.activation(places(0, 0, C), gated[:, 0:C], COPY)
         last_act = tile([N, C], F32, "act3")
         activate(last_act[:], sums[3])
-        far_acts = held([N, 3 * C], F32, "far_acts", 2)
+        far_acts = held([N, 3 * C], F32, "far_acts", 1, -1024)
         hand_on(far_acts[:, 0:HALF], far_banks[0][:].rearrange("p i c -> p (i c)"), 0)
         hand_on(far_acts[:, HALF : 3 * C], far_banks[1][:, 0, :], HALF)
-        nc.scalar.activation(places(0, C, SPLIT), gated[1], COPY)
+        nc.scalar.activation(places(0, C, SPLIT), gated[:, C:SPLIT], COPY)
         nc.vector.tensor_tensor(places(1, SPLIT, 3 * C), middle[:], gates[:, SPLIT : 3 * C], MULT)
         nc.vector.tensor_tensor(places(1, 3 * C, SLOTS), last_act[:], gates[:, 3 * C : SLOTS], MULT)
         hand_on(held([N, C], F32, "far_act3", 3, 1024)[:], far_banks[1][:, 1, :], 3 * C)

@@ -29,7 +29,7 @@ FIRST = 448
 SECOND = T - FIRST
 PAIR_SHARE = 352
 OVERLAP = 16
-LATE = 256
+LATE = 128
 SPLIT = 448
 WIDE = 1408
 
@@ -270,11 +270,12 @@ def tile_moe_loc_lin_gelu_kernel(tc, x_words, x_scales, xo, w, gate, offs, offs2
         banks = [early_bank[:, 0:C], early_bank[:, C : 2 * C]] + [psum.tile([N, C], F32, name=f"bank{b}") for b in (2, 3)]
         far_banks = []
 
-        def multiply_far(e):
-            cols = slice(e * C, (e + 1) * C)
-            second = late_codes[:] if e == E - 1 else far_codes[1][:, cols]
+        def multiply_far(first, last):
+            e = first // C
+            cols = slice(first, last)
+            second = late_codes[:] if last == SLOTS else far_codes[1][:, cols]
             product(
-                far_banks[e // 2][:, e % 2, :], e,
+                far_banks[e // 2][:, e % 2, first - e * C : last - e * C], e,
                 lambda s: second if s else far_codes[0][:, cols], lambda s: far_scales[4 * s : P, cols],
             )
 
@@ -324,8 +325,9 @@ def tile_moe_loc_lin_gelu_kernel(tc, x_words, x_scales, xo, w, gate, offs, offs2
         activate(middle[:, 2 * C - SPLIT : 3 * C - SPLIT], sums[2])
         far_banks.append(psum.tile([N, 2, C], F32, name="far_bank0", tag="shared_bank"))
         far_banks.append(psum.tile([N, 2, C], F32, name="far_bank1"))
-        for e in range(E):
-            multiply_far(e)
+        edges = [0, C, 2 * C, 3 * C, SLOTS - LATE, SLOTS]
+        for first, last in zip(edges, edges[1:]):
+            multiply_far(first, last)
         nc.scalar.activation(places(0, 0, C), gated[:, 0:C], COPY)
         last_act = tile([N, C], F32, "act3")
         activate(last_act[:], sums[3])

@@ -131,12 +131,6 @@ def tile_moe_loc_lin_gelu_kernel(tc, x_words, x_scales, xo, w, gate, offs, offs2
         raw_b0 = reuse.tile([P, 2, SECOND], F32, name="raw_b0", align_bytes=ALIGN, offset=0)
         last_raw = reuse.tile([P, 2, SECOND], F32, name="last_raw", align_bytes=ALIGN, offset=4 * woven)
 
-        def weave(s, e):
-            nc.scalar.copy(
-                x_bf[e][:, s * C * PACK : (s + 1) * C * PACK].bitcast(F32).rearrange("p (c u) -> p c u", u=2),
-                picked[s][:].bitcast(F32).rearrange("p (u c) -> p c u", u=2)[:, e * C : (e + 1) * C, :],
-            )
-
         def weave_half(s, h):
             nc.scalar.copy(
                 x_halves[h][:].bitcast(F32).rearrange("p (e s c u) -> p s e c u", e=2, s=PASSES, u=2)[:, s],
@@ -145,7 +139,7 @@ def tile_moe_loc_lin_gelu_kernel(tc, x_words, x_scales, xo, w, gate, offs, offs2
 
         def load_weights(e):
             if e == E - 1:
-                parts = [held([P, PACK, N], F32, "w_raw3_0", 1, 1024), tile([P, PACK, N], F32, "w_raw3_1")]
+                parts = [held([P, PACK, N], F32, "w_raw3_0", 1, 2048), tile([P, PACK, N], F32, "w_raw3_1")]
                 for s in range(PASSES):
                     rows = w[e, s * K_PASS : (s + 1) * K_PASS, :]
                     nc.sync.dma_start(parts[s][:], rows.rearrange("(p j) n -> p j n", j=PACK))
@@ -192,7 +186,7 @@ def tile_moe_loc_lin_gelu_kernel(tc, x_words, x_scales, xo, w, gate, offs, offs2
         planes = tile([P, T + 2 * WIDE], BF16, "planes")
         row3, pair_a = planes[:, 0:T], planes[:, T : T + 2 * WIDE]
         pair_b = tile([P, 2 * WIDE], BF16, "pair_b")[:]
-        row2 = tile([P, T], BF16, "row2")[:]
+        row2 = tile([P, WIDE], BF16, "row2")[:]
         pair_c = tile([P, 2 * T], BF16, "pair_c")[:]
         whole = [(HALF, round_on_gpsimd)]
         shared = [(SECOND - PAIR_SHARE, round_on_gpsimd), (PAIR_SHARE, round_on_scalar)]
@@ -206,8 +200,7 @@ def tile_moe_loc_lin_gelu_kernel(tc, x_words, x_scales, xo, w, gate, offs, offs2
         gather_far(scale_rows, far_scale_win[:])
         gather_far(codes0, win0[:].bitcast(U32))
 
-        gather_row(2, 0, HALF, row2)
-        gather_row(2, HALF, HALF, row2)
+        gather_row(2, 0, SLOTS, row2)
         round_row(row3, 3, [(T, round_on_gpsimd)], nc.sync)
         gather_row(3, 0, HALF, row3)
         round_pairs(pair_a, 0, 0, HALF, whole, raw_pairs("raw_a1"))
@@ -229,8 +222,7 @@ def tile_moe_loc_lin_gelu_kernel(tc, x_words, x_scales, xo, w, gate, offs, offs2
 
 
         place_scale_rows(range(0, 4))
-        for e in range(2):
-            weave(0, e)
+        weave_half(0, 0)
         round_pairs(pair_c, 1, 1, SECOND, [(FIRST, round_on_gpsimd)], raw_pairs("raw_c1", FIRST))
         round_pairs(pair_c, 1, 1, 0, shared, last_raw[:])
         gather_pairs(1, 1, pair_c, HALF)
@@ -268,14 +260,14 @@ def tile_moe_loc_lin_gelu_kernel(tc, x_words, x_scales, xo, w, gate, offs, offs2
         sums = {}
         early_bank = psum.tile([N, 2 * C], F32, name="early_bank", tag="shared_bank")
         banks = [early_bank[:, 0:C], early_bank[:, C : 2 * C]] + [psum.tile([N, C], F32, name=f"bank{b}") for b in (2, 3)]
-        far_banks = []
+        far_sums = {e: psum.tile([N, C], F32, name=f"far_bank{e}")[:] for e in (0, 3)}
 
         def multiply_far(first, last):
             e = first // C
             cols = slice(first, last)
             second = late_codes[:] if last == SLOTS else far_codes[1][:, cols]
             product(
-                far_banks[e // 2][:, e % 2, first - e * C : last - e * C], e,
+                far_sums[e][:, first - e * C : last - e * C], e,
                 lambda s: second if s else far_codes[0][:, cols], lambda s: far_scales[4 * s : P, cols],
             )
 
@@ -300,14 +292,14 @@ def tile_moe_loc_lin_gelu_kernel(tc, x_words, x_scales, xo, w, gate, offs, offs2
         weave_half(0, 1)
         late_codes = held([P, LATE], U32, "late_codes", 4)
         nc.vector.tensor_copy(late_codes[:], win1[:, 0:Q].bitcast(U32).indirect(entries(far_list, SLOTS - LATE, LATE)))
-        for e in range(2):
-            weave(1, e)
-        weave_half(1, 1)
+        for h in range(2):
+            weave_half(1, h)
         for e in range(2):
             round_weights(e, PASSES)
             quantise_weights(e)
             quantise_tokens(e)
             multiply(e)
+        multiply_far(0, C)
         quantise_tokens(2)
         round_weights(2, 0)
         quantise_weights(2)
@@ -316,28 +308,27 @@ def tile_moe_loc_lin_gelu_kernel(tc, x_words, x_scales, xo, w, gate, offs, offs2
         round_weights(3, 0)
         quantise_weights(3)
         multiply(3)
-        early = held([N, SPLIT], F32, "early_acts", 1)
+        early = held([N, SPLIT], F32, "early_acts", 1, 512)
         activate(early[:], early_bank[:, 0:SPLIT])
         gated = held([N, SPLIT], F32, "gated", 3)
         nc.vector.tensor_tensor(gated[:], early[:], gates[:, 0:SPLIT], MULT)
-        middle = held([N, 3 * C - SPLIT], F32, "middle", 1, 2048)
+        middle = held([N, 3 * C - SPLIT], F32, "middle", 1, 2304)
         activate(middle[:, 0 : 2 * C - SPLIT], sums[1][:, SPLIT - C : C])
         activate(middle[:, 2 * C - SPLIT : 3 * C - SPLIT], sums[2])
-        far_banks.append(psum.tile([N, 2, C], F32, name="far_bank0", tag="shared_bank"))
-        far_banks.append(psum.tile([N, 2, C], F32, name="far_bank1"))
-        edges = [0, C, 2 * C, 3 * C, SLOTS - LATE, SLOTS]
+        hand_on(held([N, C], F32, "far_act0", 1, 3840)[:], far_sums[0], 0)
+        far_bank = psum.tile([N, HALF], F32, name="far_bank", tag="shared_bank")
+        far_sums.update({1: far_bank[:, 0:C], 2: far_bank[:, C:HALF]})
+        edges = [C, 2 * C, 3 * C, SLOTS - LATE, SLOTS]
         for first, last in zip(edges, edges[1:]):
             multiply_far(first, last)
-        nc.scalar.activation(places(0, 0, C), gated[:, 0:C], COPY)
+        nc.scalar.activation(places(0, 0, SPLIT - C), gated[:, 0 : SPLIT - C], COPY)
         last_act = tile([N, C], F32, "act3")
         activate(last_act[:], sums[3])
-        far_acts = held([N, 3 * C], F32, "far_acts", 1, -1024)
-        hand_on(far_acts[:, 0:HALF], far_banks[0][:].rearrange("p i c -> p (i c)"), 0)
-        hand_on(far_acts[:, HALF : 3 * C], far_banks[1][:, 0, :], HALF)
-        nc.scalar.activation(places(0, C, SPLIT), gated[:, C:SPLIT], COPY)
+        hand_on(held([N, HALF], F32, "far_act12", 1, 256)[:], far_bank[:], C)
         nc.vector.tensor_tensor(places(1, SPLIT, 3 * C), middle[:], gates[:, SPLIT : 3 * C], MULT)
-        nc.vector.tensor_tensor(places(1, 3 * C, SLOTS), last_act[:], gates[:, 3 * C : SLOTS], MULT)
-        hand_on(held([N, C], F32, "far_act3", 3, 1024)[:], far_banks[1][:, 1, :], 3 * C)
+        nc.scalar.activation(places(1, SPLIT - C, SPLIT), gated[:, SPLIT - C : SPLIT], COPY)
+        nc.vector.tensor_tensor(places(0, 3 * C, SLOTS), last_act[:], gates[:, 3 * C : SLOTS], MULT)
+        hand_on(held([N, C], F32, "far_act3", 3, 1024)[:], far_sums[3], 3 * C)
         for h in range(2):
             cols = slice(h * HALF, (h + 1) * HALF)
             own = tile([P, HALF], F32, f"own{h}")

from contextlib import ExitStack

import concourse.mybir as mybir

K, T, Q, E, C, N = 1024, 1024, 768, 4, 256, 128
FLOPS = 2 * K * N * 2 * E * C

F32 = mybir.dt.float32
BF16 = mybir.dt.bfloat16
I32 = mybir.dt.int32
U32 = mybir.dt.uint32
U16 = mybir.dt.uint16
U8 = mybir.dt.uint8
FP8X4 = mybir.dt.float8_e4m3fn_x4
GELU = mybir.ActivationFunctionType.Gelu_apprx_tanh
COPY = mybir.ActivationFunctionType.Copy
MULT = mybir.AluOpType.mult
ADD = mybir.AluOpType.add

P = 128
PACK = 4
K_PASS = P * PACK
PASSES = K // K_PASS
SLOTS = E * C
HALF = 512
ALIGN = 256
ROW_SHARE = 640
FIRST = 448
SECOND = T - FIRST
PAIR_SHARE = 352
OVERLAP = 16
LATE = 128
SPLIT = 448
WIDE = 1408


def tile_moe_loc_lin_gelu_kernel(tc, x_words, x_scales, xo, w, gate, offs, offs2, out):
    nc = tc.nc
    with ExitStack() as ctx:
        keep = ctx.enter_context(tc.tile_pool(name="keep", bufs=1))
        reuse = ctx.enter_context(tc.tile_pool(name="reuse", bufs=1))
        chain = ctx.enter_context(tc.tile_pool(name="chain", bufs=1))
        psum = ctx.enter_context(tc.psum_pool(name="psum", bufs=1))

        def tile(shape, dtype, name, tag=None):
            return keep.tile(shape, dtype, name=name, tag=tag or name, align_bytes=ALIGN)

        def entries(lst, first, count):
            return lst[:, first // 16 : (first + count) // 16]

        own_list = keep.tile([P, SLOTS // 16], U16, name="own_list")
        far_list = keep.tile([P, SLOTS // 16], U16, name="far_list")

        zero = keep.tile([P, 8], F32, name="zero")

        far_scale_win = tile([P, WIDE], U8, "far_scale_win")
        nc.vector.memset(zero[:], 0.0)
        nc.vector.memset(far_scale_win[32:64, 0:Q].bitcast(I32), 0)
        nc.vector.memset(far_scale_win[64:P, 0:Q].bitcast(I32), 0)
        far_scales = tile([P, SLOTS], U8, "far_scales")
        nc.vector.memset(far_scales[:].bitcast(I32), 0)
        windows = [tile([P, T], F32, f"window{i}") for i in range(2)]
        nc.scalar.activation(windows[0][:], zero[:, 0:1].to_broadcast([P, T]), GELU)
        nc.vector.memset(windows[1][:].bitcast(I32), 0)

        def gather_far(dst, window, slots=SLOTS):
            nc.vector.tensor_copy(dst[:, 0:slots], window.indirect(entries(far_list, 0, slots)))

        def far_words(s):
            win = tile([P, WIDE], I32, f"far_word_win{s}")
            nc.sync.dma_start(win[:, 0:Q], x_words[s].rearrange("p t d -> p (t d)").bitcast(I32))
            codes = tile([P, SLOTS], U32, f"far_codes{s}")
            return win, codes

        def round_on_scalar(dst, src):
            nc.scalar.copy(dst, src)

        def round_on_gpsimd(dst, src):
            nc.gpsimd.tensor_scalar(dst, src, 1.0, 0.0, MULT, ADD)

        def pass_rows(s):
            return xo[s * K_PASS : (s + 1) * K_PASS, :].rearrange("(p j) t -> p j t", j=PACK)

        def held(shape, dtype, name, stage, at=0):
            return chain.tile(shape, dtype, name=name, align_bytes=ALIGN, offset=8192 * stage + at)

        picked_early = held([P, 4 * SLOTS], BF16, "picked0", 4)
        picked = [picked_early, tile([P, 4 * SLOTS], BF16, "picked1")]

        def round_pairs(pairs, s, u, first, shares, raw):
            nc.sync.dma_start(raw, pass_rows(s)[:, 2 * u : 2 * u + 2, first : first + raw.shape[2]])
            done = 0
            for count, rounder in shares:
                rounder(
                    pairs[:, 2 * (first + done) : 2 * (first + done + count)].rearrange("p (t j) -> p t j", j=2),
                    raw[:, :, done : done + count].rearrange("p j t -> p t j"),
                )
                done += count

        def raw_pairs(name, count=HALF):
            return tile([P, 2, count], F32, name)[:]

        def gather_pairs(s, u, pairs, count):
            for first in range(0, SLOTS, count):
                nc.vector.tensor_copy(
                    picked[s][:].bitcast(U32)[:, u * SLOTS + first : u * SLOTS + first + count],
                    pairs.bitcast(U32).indirect(entries(own_list, first, count)),
                )

        def round_row(row, j, shares, queue):
            raw = tile([P, T], F32, f"raw_row{j}")
            queue.dma_start(raw[:], pass_rows(0)[:, j, :])
            done = 0
            for count, rounder in shares:
                rounder(row[:, done : done + count], raw[:, done : done + count])
                done += count

        def gather_row(j, first, count, window):
            start = 2 * (SLOTS + first)
            nc.scalar.activation(
                picked_early[:, start + j % 2 : start + 2 * count : 2],
                window.indirect(entries(own_list, first, count)),
                COPY,
            )

        woven = PASSES * C * PACK
        x_halves = [
            reuse.tile([P, 2 * woven], BF16, name=f"x_half{h}", align_bytes=ALIGN, offset=4 * woven * h) for h in range(2)
        ]
        x_bf = {e: x_halves[e // 2][:, e % 2 * woven : (e % 2 + 1) * woven] for e in range(E)}
        raw_b0 = reuse.tile([P, 2, SECOND], F32, name="raw_b0", align_bytes=ALIGN, offset=0)
        last_raw = reuse.tile([P, 2, SECOND], F32, name="last_raw", align_bytes=ALIGN, offset=4 * woven)

        def weave_half(s, h):
            nc.scalar.copy(
                x_halves[h][:].bitcast(F32).rearrange("p (e s c u) -> p s e c u", e=2, s=PASSES, u=2)[:, s],
                picked[s][:].bitcast(F32).rearrange("p (u h e c) -> p h e c u", u=2, h=2, e=2)[:, h],
            )

        def load_weights(e):
            if e == E - 1:
                parts = [held([P, PACK, N], F32, "w_raw3_0", 1, 2048), tile([P, PACK, N], F32, "w_raw3_1")]
                for s in range(PASSES):
                    rows = w[e, s * K_PASS : (s + 1) * K_PASS, :]
                    nc.sync.dma_start(parts[s][:], rows.rearrange("(p j) n -> p j n", j=PACK))
                return parts
            if e == 2:
                w_raw = held([P, PASSES, PACK, N], F32, f"w_raw{e}", 2)
            else:
                w_raw = tile([P, PASSES, PACK, N], F32, f"w_raw{e}")
            nc.sync.dma_start(w_raw[:], w[e].rearrange("(s p j) n -> p s j n", s=PASSES, j=PACK))
            return w_raw

        weights = {}

        w_bfs = {}

        def round_weights(e, passes_on_gpsimd):
            w_raw = w_raws[e]
            w_bf = held([P, PASSES, N, PACK], BF16, f"w_bf{e}", 0, (3072, 6144, 2048, 4096)[e])
            if passes_on_gpsimd:
                round_on_gpsimd(
                    w_bf[:, 0:passes_on_gpsimd, :, :], w_raw[:, 0:passes_on_gpsimd, :, :].rearrange("p s j n -> p s n j")
                )
            elif e == E - 1:
                for s in range(PASSES):
                    round_on_scalar(
                        w_bf[:, s, :, :].rearrange("p (c i) j -> p c j i", i=4),
                        w_raw[s][:].rearrange("p j (c i) -> p c j i", i=4),
                    )
            else:
                round_on_scalar(
                    w_bf[:].rearrange("p s (c i) j -> p s c j i", i=4), w_raw[:].rearrange("p s j (c i) -> p s c j i", i=4)
                )
            w_bfs[e] = w_bf

        def quantise_weights(e):
            w_bf = w_bfs[e]
            w_codes = tile([P, PASSES * N], U32, f"w_codes{e}")
            w_scales = tile([P, PASSES * N], U8, f"w_scales{e}")
            nc.vector.quantize_mx(
                out=w_codes[:].bitcast(FP8X4), scales=w_scales[:], in_=w_bf[:].rearrange("p s n j -> p (s n j)")
            )
            weights[e] = (w_codes, w_scales)

        planes = tile([P, T + 2 * WIDE], BF16, "planes")
        row3, pair_a = planes[:, 0:T], planes[:, T : T + 2 * WIDE]
        pair_b = tile([P, 2 * WIDE], BF16, "pair_b")[:]
        row2 = tile([P, WIDE], BF16, "row2")[:]
        pair_c = tile([P, 2 * T], BF16, "pair_c")[:]
        whole = [(HALF, round_on_gpsimd)]
        shared = [(SECOND - PAIR_SHARE, round_on_gpsimd), (PAIR_SHARE, round_on_scalar)]

        nc.sync.dma_start(far_list[:], offs2)
        nc.sync.dma_start(far_scale_win[0:32, 0:Q].bitcast(I32), x_scales.rearrange("s b t -> (s b) t").bitcast(I32))
        round_row(row2, 2, [(ROW_SHARE, round_on_scalar), (T - ROW_SHARE, round_on_gpsimd)], nc.sync)
        nc.sync.dma_start(own_list[:], offs)
        win0, codes0 = far_words(0)
        scale_rows = tile([P, SLOTS], U8, "scale_rows")
        gather_far(scale_rows, far_scale_win[:])
        gather_far(codes0, win0[:].bitcast(U32))

        gather_row(2, 0, SLOTS, row2)
        round_row(row3, 3, [(T, round_on_gpsimd)], nc.sync)
        gather_row(3, 0, HALF, row3)
        round_pairs(pair_a, 0, 0, HALF, whole, raw_pairs("raw_a1"))
        win1, codes1 = far_words(1)
        gather_far(codes1, win1[:].bitcast(U32), SLOTS - LATE)
        far_codes = [codes0, codes1]
        round_pairs(pair_a, 0, 0, 0, [(C, round_on_gpsimd), (C, round_on_scalar)], raw_pairs("raw_a0"))
        gather_pairs(0, 0, pair_a[:, 0 : 2 * T], HALF)
        gather_row(3, HALF, HALF, planes[:, 0 : T + OVERLAP])
        round_pairs(pair_b, 1, 0, SECOND, [(FIRST, round_on_gpsimd)], raw_pairs("raw_b1", FIRST))
        round_pairs(pair_b, 1, 0, 0, shared, raw_b0[:])
        gather_pairs(1, 0, pair_b, SLOTS)

        def place_scale_rows(blocks):
            for block in blocks:
                s, quad = divmod(block, 4)
                to, src = 32 * quad + 4 * s, 4 * block
                nc.sync.dma_start(far_scales[to : to + 4, :].bitcast(I32), scale_rows[src : src + 4, :].bitcast(I32))


        place_scale_rows(range(0, 4))
        weave_half(0, 0)
        round_pairs(pair_c, 1, 1, SECOND, [(FIRST, round_on_gpsimd)], raw_pairs("raw_c1", FIRST))
        round_pairs(pair_c, 1, 1, 0, shared, last_raw[:])
        gather_pairs(1, 1, pair_c, HALF)

        w_raws = [load_weights(e) for e in range(2)]
        place_scale_rows(range(4, 8))
        w_raws.extend(load_weights(e) for e in range(2, E))
        gates = tile([P, SLOTS], F32, "gates")
        nc.sync.dma_start(gates[:], gate)

        def product(acc, e, codes, scales):
            w_codes, w_scales = weights[e]
            for s in range(PASSES):
                nc.tensor.matmul_mx(
                    out=acc,
                    lhsT=w_codes[:, s * N : (s + 1) * N].bitcast(FP8X4),
                    lhsT_scale=w_scales[:, s * N : (s + 1) * N],
                    rhs=codes(s).bitcast(FP8X4),
                    rhs_scale=scales(s),
                    start=(s == 0),
                    stop=(s == PASSES - 1),
                )

        tokens = {}

        def quantise_tokens(e):
            if e == E - 1:
                x_codes = held([P, PASSES * C], U32, f"x_codes{e}", 2)
            else:
                x_codes = tile([P, PASSES * C], U32, f"x_codes{e}")
            x_planes = tile([P, PASSES * C], U8, f"x_planes{e}")
            nc.vector.quantize_mx(out=x_codes[:].bitcast(FP8X4), scales=x_planes[:], in_=x_bf[e])
            tokens[e] = (x_codes, x_planes)

        sums = {}
        early_bank = psum.tile([N, 2 * C], F32, name="early_bank", tag="shared_bank")
        banks = [early_bank[:, 0:C], early_bank[:, C : 2 * C]] + [psum.tile([N, C], F32, name=f"bank{b}") for b in (2, 3)]
        far_sums = {e: psum.tile([N, C], F32, name=f"far_bank{e}")[:] for e in (0, 3)}

        def multiply_far(first, last):
            e = first // C
            cols = slice(first, last)
            second = late_codes[:] if last == SLOTS else far_codes[1][:, cols]
            product(
                far_sums[e][:, first - e * C : last - e * C], e,
                lambda s: second if s else far_codes[0][:, cols], lambda s: far_scales[4 * s : P, cols],
            )

        def multiply(e):
            x_codes, x_planes = tokens[e]
            sums[e] = banks[e][:]
            product(
                sums[e], e,
                lambda s: x_codes[:, s * C : (s + 1) * C], lambda s: x_planes[:, s * C : (s + 1) * C],
            )

        def activate(act, sums_in):
            nc.scalar.activation(act, sums_in, GELU)

        def places(window, first, last):
            return windows[window][:].indirect(entries(own_list, first, last - first))

        def hand_on(act, sums_in, first):
            nc.scalar.activation(act, sums_in, GELU)
            nc.sync.dma_start(out[:, T + first : T + first + act.shape[1]], act)

        weave_half(0, 1)
        late_codes = held([P, LATE], U32, "late_codes", 4)
        nc.vector.tensor_copy(late_codes[:], win1[:, 0:Q].bitcast(U32).indirect(entries(far_list, SLOTS - LATE, LATE)))
        for h in range(2):
            weave_half(1, h)
        for e in range(2):
            round_weights(e, PASSES)
            quantise_weights(e)
            quantise_tokens(e)
            multiply(e)
        multiply_far(0, C)
        quantise_tokens(2)
        round_weights(2, 0)
        quantise_weights(2)
        multiply(2)
        quantise_tokens(3)
        round_weights(3, 0)
        quantise_weights(3)
        multiply(3)
        early = held([N, SPLIT], F32, "early_acts", 1, 512)
        activate(early[:], early_bank[:, 0:SPLIT])
        gated = held([N, SPLIT], F32, "gated", 3)
        nc.vector.tensor_tensor(gated[:], early[:], gates[:, 0:SPLIT], MULT)
        middle = held([N, 3 * C - SPLIT], F32, "middle", 1, 2304)
        activate(middle[:, 0 : 2 * C - SPLIT], sums[1][:, SPLIT - C : C])
        activate(middle[:, 2 * C - SPLIT : 3 * C - SPLIT], sums[2])
        hand_on(held([N, C], F32, "far_act0", 1, 3840)[:], far_sums[0], 0)
        far_bank = psum.tile([N, HALF], F32, name="far_bank", tag="shared_bank")
        far_sums.update({1: far_bank[:, 0:C], 2: far_bank[:, C:HALF]})
        edges = [C, 2 * C, 3 * C, SLOTS - LATE, SLOTS]
        for first, last in zip(edges, edges[1:]):
            multiply_far(first, last)
        nc.scalar.activation(places(0, 0, SPLIT - C), gated[:, 0 : SPLIT - C], COPY)
        last_act = tile([N, C], F32, "act3")
        activate(last_act[:], sums[3])
        hand_on(held([N, HALF], F32, "far_act12", 1, 256)[:], far_bank[:], C)
        nc.vector.tensor_tensor(places(1, SPLIT, 3 * C), middle[:], gates[:, SPLIT : 3 * C], MULT)
        nc.scalar.activation(places(1, SPLIT - C, SPLIT), gated[:, SPLIT - C : SPLIT], COPY)
        nc.vector.tensor_tensor(places(0, 3 * C, SLOTS), last_act[:], gates[:, 3 * C : SLOTS], MULT)
        hand_on(held([N, C], F32, "far_act3", 3, 1024)[:], far_sums[3], 3 * C)
        for h in range(2):
            cols = slice(h * HALF, (h + 1) * HALF)
            own = tile([P, HALF], F32, f"own{h}")
            nc.vector.tensor_tensor(own[:], windows[0][:, cols], windows[1][:, cols], ADD)
            nc.sync.dma_start(out[:, cols], own[:])
